import numpy as np
import ml_dtypes


def mxq(x, axis, fmt="e4m3"):
    dtype, down = {"e4m3": (ml_dtypes.float8_e4m3fn, 7), "e5m2": (ml_dtypes.float8_e5m2, 14)}[fmt]
    v = np.moveaxis(np.asarray(x, np.float32).astype(ml_dtypes.bfloat16).astype(np.float64), axis, -1)
    blocks = v.reshape(v.shape[:-1] + (-1, 32))
    amax = np.abs(blocks).max(-1, keepdims=True)
    byte = np.maximum(np.where(amax > 0, np.frexp(amax)[1] - 1 + 127, 0) - down, 1)
    scale = np.exp2(byte - 127.0)
    codes = (blocks / scale).astype(np.float32).astype(dtype).astype(np.float64)
    return np.moveaxis((codes * scale).reshape(v.shape), -1, axis)


WIDE = False


def mx_kscale(k):
    if not WIDE:
        return np.ones(k)
    levels = np.array([10, -10, 5, -5, 0])
    if k % 512:
        return np.exp2(np.random.permutation(np.resize(levels, k // 32))).repeat(32)
    a = np.empty((k // 512, 16))
    for p in range(k // 512):
        a[p, :8] = np.random.permutation(np.resize(levels, 8))
        for g in range(8):
            far = levels[np.abs(levels - a[p, g]) >= 10]
            a[p, g + 8] = far[np.random.randint(len(far))]
    return np.exp2(a.ravel()).repeat(32)


def f64(x):
    return np.asarray(x).astype(np.float64)


def striped(idx):
    return np.tile(idx.reshape(-1, 16).T, (8, 1)).astype(np.uint16)


def unstriped(offs):
    return offs[:16].T.reshape(-1).astype(np.int64)


def pack_weight(w):
    k, n = w.shape
    w = f64(np.asarray(w, np.float32).astype(ml_dtypes.bfloat16)).reshape(k // 32, 32, n)
    amax = np.abs(w).max(1)
    byte = np.clip(np.where(amax > 0, np.frexp(amax)[1] - 1 + 127 - 7, 1), 1, 254)
    scaled = (w * np.exp2(127.0 - byte)[:, None, :]).reshape(k, n).astype(np.float32)
    words = np.ascontiguousarray(scaled.reshape(k // 512, 128, 4, n).transpose(0, 1, 3, 2)).astype(ml_dtypes.float8_e4m3fn).view(np.uint8)
    return words, np.ascontiguousarray(byte.astype(np.uint8).reshape(k // 512, 16, n))


def unpack_weight(words, scales):
    g, p, n, _ = words.shape
    vals = np.ascontiguousarray(words).view(ml_dtypes.float8_e4m3fn).astype(np.float64) * np.repeat(np.exp2(scales.astype(np.float64) - 127.0), 8, axis=1)[..., None]
    return vals.transpose(0, 1, 3, 2).reshape(g * 512, n)


def silu(v):
    return v / (1.0 + np.exp(-np.maximum(v, -700.0)))


K, T, N = 1536, 512, 256


def setup_inputs():
    n = np.random.standard_normal
    s = mx_kscale(K)[:, None]
    idx = np.random.permutation(K)
    x = n((T, K))
    x[:, idx] *= s[:, 0]
    words, scales = pack_weight(n((K, N)) / np.sqrt(K) / s)
    return {
        "x": x.astype(np.float32),
        "w_words": words,
        "w_scales": scales,
        "b": (0.3 * n((N, 1))).astype(np.float32),
        "offs": striped(idx),
    }


def reference(x, w_words, w_scales, b, offs):
    w = unpack_weight(w_words, w_scales)
    idx = unstriped(offs)
    xq = mxq(f64(x)[:, idx], 1, "e4m3").T
    return silu((w.T @ xq) + f64(b))

@@ -1,0 +1,156 @@
+from contextlib import ExitStack
+
+import concourse.mybir as mybir
+from concourse.masks import make_identity
+
+K, T, N = 1536, 512, 256
+FLOPS = 2 * K * T * N
+
+F32 = mybir.dt.float32
+BF16 = mybir.dt.bfloat16
+U32 = mybir.dt.uint32
+I32 = mybir.dt.int32
+U16 = mybir.dt.uint16
+U8 = mybir.dt.uint8
+FP8X4 = mybir.dt.float8_e4m3fn_x4
+COPY = mybir.ActivationFunctionType.Copy
+SILU = mybir.ActivationFunctionType.Silu
+MULT = mybir.AluOpType.mult
+ADD = mybir.AluOpType.add
+
+P = 128
+PASSES = K // 512
+HALVES = T // 256
+CUTS = [[0, 576, 1152, 1536], [0, 576, 1152, 1536]]
+
+
+def tile_picked_actorder_lin_silu_perm_l_kernel(tc, x, w_words, w_scales, b, offs, out):
+    nc = tc.nc
+    with ExitStack() as ctx:
+        keep = ctx.enter_context(tc.tile_pool(name="keep", bufs=1))
+        turn = ctx.enter_context(tc.psum_pool(name="turn", bufs=4))
+        accs = ctx.enter_context(tc.psum_pool(name="accs", bufs=1))
+
+        offsets = keep.tile([P, K // 16], U16, name="offsets")
+        ident = keep.tile([P, P], F32, name="ident")
+        w_codes = keep.tile([P, PASSES, N], U32, name="w_codes", align_bytes=64)
+        w_planes = keep.tile([P, PASSES, N], U8, name="w_planes", align_bytes=64)
+        bias = keep.tile([P, 2], F32, name="bias")
+        warm = keep.tile([P, 1], F32, name="warm")
+        warm2 = keep.tile([P, 1], F32, name="warm2")
+
+        raws = {}
+        pairs = []
+        for h in range(HALVES):
+            pairs.append(keep.tile([P, 2 * K], BF16, name=f"pairs{h}", align_bytes=64))
+            for c in range(3):
+                raws[h, c] = keep.tile([P, 2, CUTS[h][c + 1] - CUTS[h][c]], F32, name=f"raw{h}_{c}")
+
+        def load_x(h, c):
+            nc.sync.dma_start(
+                raws[h, c][:],
+                x[256 * h : 256 * (h + 1), CUTS[h][c] : CUTS[h][c + 1]].rearrange("(e p) c -> p e c", e=2),
+            )
+
+        load_x(0, 0)
+        nc.sync.dma_start(offsets[:], offs)
+        load_x(0, 1)
+        load_x(0, 2)
+        load_x(1, 0)
+        load_x(1, 1)
+        load_x(1, 2)
+        nc.sync.dma_start(w_codes[:].bitcast(I32), w_words.rearrange("a p n r -> p a (n r)").bitcast(I32))
+        nc.vector.memset(w_planes[:].bitcast(U32), 0)
+        for q in range(4):
+            nc.sync.dma_start(
+                w_planes[32 * q : 32 * q + 4, :, :].bitcast(I32),
+                w_scales[:, 4 * q : 4 * q + 4, :].rearrange("a q n -> q a n").bitcast(I32),
+            )
+        nc.sync.dma_start(bias[:], b.rearrange("(m p) o -> p (m o)", p=P))
+
+        nc.vector.memset(warm[:], 0.0)
+        nc.scalar.activation(warm2[:], warm[:], SILU)
+        make_identity(nc, ident[:])
+
+        def cast(engine, h, c, lo, hi):
+            src = raws[h, c][:, :, lo:hi].rearrange("p e c -> p c e")
+            dst = pairs[h][:, 2 * (CUTS[h][c] + lo) : 2 * (CUTS[h][c] + hi)].rearrange("p (c e) -> p c e", e=2)
+            if engine == "v":
+                nc.vector.tensor_copy(dst, src)
+            elif engine == "s":
+                nc.scalar.copy(dst, src)
+            else:
+                nc.gpsimd.tensor_scalar(dst, src, 1.0, 0.0, MULT, ADD)
+
+        def acc_tile(h, m):
+            return accs.tile([P, 256], F32, name=f"acc{h}{m}")
+
+        acc = {(h, m): acc_tile(h, m) for h in range(HALVES) for m in range(2)}
+
+        def gather(h, g):
+            picked = keep.tile([P, 1024], BF16, name=f"picked{h}{g}", align_bytes=64)
+            words = picked[:].bitcast(U32)
+            nc.vector.tensor_copy(
+                words.rearrange("p (t q) -> p q t", t=4) if (h, g) == (1, 2) else words,
+                pairs[h][:].bitcast(U32).indirect(offsets[:, 32 * g : 32 * (g + 1)]),
+            )
+            return picked
+
+        grouped = {}
+
+        def turn_over(h, g):
+            bank = turn.tile([P, 512], F32, name="bank")
+            words = picks[h, g][:].bitcast(F32)
+            for t in range(4):
+                nc.tensor.transpose(bank[:, P * t : P * (t + 1)], words[:, P * t : P * (t + 1)] if (h, g) == (1, 2) else words[:, t : 512 : 4], ident[:])
+            src = bank[:].bitcast(BF16).rearrange("p (t q e) -> p e q t", t=4, e=2)
+            grouped[h, g] = keep.tile([P, 1024], BF16, name=f"grouped{h}{g}", align_bytes=64)
+            dst = grouped[h, g][:].rearrange("p (e q t) -> p e q t", e=2, t=4)
+            if (h, g) in [(1, 2)]:
+                for e in range(2):
+                    nc.scalar.copy(dst[:, e], src[:, e])
+            else:
+                nc.scalar.copy(dst, src)
+
+        def multiply(h, g):
+            codes = keep.tile([P, 256], U32, name=f"codes{h}{g}", align_bytes=64)
+            planes = keep.tile([P, 256], U8, name=f"planes{h}{g}", align_bytes=64)
+            for e in range(2) if (h, g) in [(1, 2)] else [slice(0, 2)]:
+                lo, hi = (e.start, e.stop) if (h, g) not in [(1, 2)] else (e, e + 1)
+                half = slice(P * lo, P * hi)
+                nc.vector.quantize_mx(out=codes[:, half].bitcast(FP8X4), scales=planes[:, half], in_=grouped[h, g][:, 512 * lo : 512 * hi])
+            for m in range(2):
+                cols = slice(P * m, P * (m + 1))
+                nc.tensor.matmul_mx(
+                    out=acc[h, m][:],
+                    lhsT=w_codes[:, g, cols].bitcast(FP8X4),
+                    lhsT_scale=w_planes[:, g, cols],
+                    rhs=codes[:].bitcast(FP8X4),
+                    rhs_scale=planes[:],
+                    start=(g == 0),
+                    stop=(g == PASSES - 1),
+                )
+
+        cast("v", 0, 0, 0, 576)
+        cast("v", 0, 1, 0, 576)
+        cast("v", 0, 2, 0, 256)
+        cast("s", 0, 2, 256, 384)
+        cast("s", 1, 0, 0, 576)
+        cast("s", 1, 1, 0, 192)
+        cast("s", 1, 2, 0, 256)
+
+        picks = {(0, g): gather(0, g) for g in range(PASSES)}
+        cast("v", 1, 1, 192, 576)
+        cast("v", 1, 2, 256, 384)
+        for g in range(PASSES):
+            picks[1, g] = gather(1, g)
+        for h in range(HALVES):
+            for g in range(PASSES):
+                turn_over(h, g)
+        for h in range(HALVES):
+            for g in range(PASSES):
+                multiply(h, g)
+            for m in range(2):
+                y = keep.tile([P, 256], F32, name=f"y{h}{m}")
+                nc.scalar.activation(y[:], acc[h, m][:], SILU, bias=bias[:, m : m + 1])
+                nc.sync.dma_start(out[P * m : P * (m + 1), 256 * h : 256 * (h + 1)], y[:])

@@ -13,7 +13,6 @@ I32 = mybir.dt.int32
 U16 = mybir.dt.uint16
 U8 = mybir.dt.uint8
 FP8X4 = mybir.dt.float8_e4m3fn_x4
-COPY = mybir.ActivationFunctionType.Copy
 SILU = mybir.ActivationFunctionType.Silu
 MULT = mybir.AluOpType.mult
 ADD = mybir.AluOpType.add
@@ -21,15 +20,19 @@ ADD = mybir.AluOpType.add
 P = 128
 PASSES = K // 512
 HALVES = T // 256
-CUTS = [[0, 576, 1152, 1536], [0, 576, 1152, 1536]]
+CUTS = [[0,512,1024,1536],[0,512,1024,1536]]
+CASTS = [[[["s",0,512]],[["g",0,512]],[["s",0,512]]],[[["s",0,512]],[["g",0,512]],[["g",0,192],["s",192,512]]]]
+FOUR = [[1,1,1],[4,4,4]]
+HALFTAG = [["bank00", "acc0"]]
+HOLD = 2
 
 
 def tile_picked_actorder_lin_silu_perm_l_kernel(tc, x, w_words, w_scales, b, offs, out):
     nc = tc.nc
     with ExitStack() as ctx:
         keep = ctx.enter_context(tc.tile_pool(name="keep", bufs=1))
-        turn = ctx.enter_context(tc.psum_pool(name="turn", bufs=4))
-        accs = ctx.enter_context(tc.psum_pool(name="accs", bufs=1))
+        psum = ctx.enter_context(tc.psum_pool(name="psum", bufs=1))
+        shared = ctx.enter_context(tc.tile_pool(name="shared", bufs=1))
 
         offsets = keep.tile([P, K // 16], U16, name="offsets")
         ident = keep.tile([P, P], F32, name="ident")
@@ -39,12 +42,18 @@ def tile_picked_actorder_lin_silu_perm_l_kernel(tc, x, w_words, w_scales, b, off
         warm = keep.tile([P, 1], F32, name="warm")
         warm2 = keep.tile([P, 1], F32, name="warm2")
 
+        rows0 = keep.tile([P, 2, K], F32, name="rows0", align_bytes=64)
         raws = {}
         pairs = []
         for h in range(HALVES):
-            pairs.append(keep.tile([P, 2 * K], BF16, name=f"pairs{h}", align_bytes=64))
-            for c in range(3):
-                raws[h, c] = keep.tile([P, 2, CUTS[h][c + 1] - CUTS[h][c]], F32, name=f"raw{h}_{c}")
+            pairs.append(keep.tile([P, 2 * K], BF16, name=f"pairs{h}", tag=f"pairs{h}", align_bytes=64))
+            for c in range(len(CUTS[h]) - 1):
+                if h == 0:
+                    raws[h, c] = rows0[:, :, CUTS[h][c] : CUTS[h][c + 1]]
+                elif (h, c) == (1, HOLD):
+                    raws[h, c] = shared.tile([P, 2, CUTS[h][c + 1] - CUTS[h][c]], F32, name=f"raw{h}_{c}", align_bytes=64, offset=3072)
+                else:
+                    raws[h, c] = keep.tile([P, 2, CUTS[h][c + 1] - CUTS[h][c]], F32, name=f"raw{h}_{c}", align_bytes=64)
 
         def load_x(h, c):
             nc.sync.dma_start(
@@ -52,13 +61,12 @@ def tile_picked_actorder_lin_silu_perm_l_kernel(tc, x, w_words, w_scales, b, off
                 x[256 * h : 256 * (h + 1), CUTS[h][c] : CUTS[h][c + 1]].rearrange("(e p) c -> p e c", e=2),
             )
 
-        load_x(0, 0)
+        nc.sync.dma_start(rows0[:, 0, :], x[0:P, :])
         nc.sync.dma_start(offsets[:], offs)
-        load_x(0, 1)
-        load_x(0, 2)
-        load_x(1, 0)
-        load_x(1, 1)
-        load_x(1, 2)
+        for c in range(len(CUTS[0]) - 1):
+            nc.sync.dma_start(rows0[:, 1, CUTS[0][c] : CUTS[0][c + 1]], x[P : 2 * P, CUTS[0][c] : CUTS[0][c + 1]])
+        for c in range(len(CUTS[1]) - 1):
+            load_x(1, c)
         nc.sync.dma_start(w_codes[:].bitcast(I32), w_words.rearrange("a p n r -> p a (n r)").bitcast(I32))
         nc.vector.memset(w_planes[:].bitcast(U32), 0)
         for q in range(4):
@@ -72,85 +80,158 @@ def tile_picked_actorder_lin_silu_perm_l_kernel(tc, x, w_words, w_scales, b, off
         nc.scalar.activation(warm2[:], warm[:], SILU)
         make_identity(nc, ident[:])
 
-        def cast(engine, h, c, lo, hi):
-            src = raws[h, c][:, :, lo:hi].rearrange("p e c -> p c e")
-            dst = pairs[h][:, 2 * (CUTS[h][c] + lo) : 2 * (CUTS[h][c] + hi)].rearrange("p (c e) -> p c e", e=2)
-            if engine == "v":
-                nc.vector.tensor_copy(dst, src)
-            elif engine == "s":
-                nc.scalar.copy(dst, src)
-            else:
-                nc.gpsimd.tensor_scalar(dst, src, 1.0, 0.0, MULT, ADD)
+        def cast(h, c):
+            for engine, lo, hi in CASTS[h][c]:
+                src = raws[h, c][:, :, lo:hi].rearrange("p e c -> p c e")
+                dst = pairs[h][:, 2 * (CUTS[h][c] + lo) : 2 * (CUTS[h][c] + hi)].rearrange("p (c e) -> p c e", e=2)
+                if engine == "v":
+                    nc.vector.tensor_copy(dst, src)
+                elif engine == "s":
+                    nc.scalar.copy(dst, src)
+                else:
+                    nc.gpsimd.tensor_scalar(dst, src, 1.0, 0.0, MULT, ADD)
 
-        def acc_tile(h, m):
-            return accs.tile([P, 256], F32, name=f"acc{h}{m}")
+        PLACE = {"grouped02": 2048, "grouped01": 6144, "grouped12e0": 9216, "y00": 8704, "y01": 9728}
 
-        acc = {(h, m): acc_tile(h, m) for h in range(HALVES) for m in range(2)}
+        def place(name, cols):
+            if name in PLACE:
+                return shared.tile([P, cols], BF16, name=name, align_bytes=64, offset=PLACE[name])
+            return keep.tile([P, cols], BF16, name=name, align_bytes=64)
+
+        picks = {}
+        banks = {}
+        grouped = {}
+        codes = {}
+        planes = {}
+        acc = {}
 
         def gather(h, g):
-            picked = keep.tile([P, 1024], BF16, name=f"picked{h}{g}", align_bytes=64)
-            words = picked[:].bitcast(U32)
+            picks[h, g] = place(f"picked{h}{g}", 1024)
+            words = picks[h, g][:].bitcast(U32)
+            if FOUR[h][g] == 4:
+                words = words.rearrange("p (t q) -> p q t", t=4)
+            elif FOUR[h][g] == 2:
+                words = words.rearrange("p (u q f) -> p q u f", u=2, f=2)
+            nc.vector.tensor_copy(words, pairs[h][:].bitcast(U32).indirect(offsets[:, 32 * g : 32 * (g + 1)]))
+
+        def gather_alone(e, g):
+            picks[0, g, e] = place(f"alone{g}{e}", 512)
             nc.vector.tensor_copy(
-                words.rearrange("p (t q) -> p q t", t=4) if (h, g) == (1, 2) else words,
-                pairs[h][:].bitcast(U32).indirect(offsets[:, 32 * g : 32 * (g + 1)]),
+                picks[0, g, e][:].rearrange("p (u q f) -> p q u f", u=2, f=2),
+                rows0[:, e, :].indirect(offsets[:, 32 * g : 32 * (g + 1)]),
             )
-            return picked
 
-        grouped = {}
+        def turn_alone(e, g):
+            banks[0, g, e] = psum.tile([P, 256], F32, name=f"half{g}{e}", tag=HALFTAG[g][e])
+            words = picks[0, g, e][:].bitcast(F32)
+            for u in range(2):
+                nc.tensor.transpose(banks[0, g, e][:, P * u : P * (u + 1)], words[:, P * u : P * (u + 1)], ident[:])
 
-        def turn_over(h, g):
-            bank = turn.tile([P, 512], F32, name="bank")
+        def empty_alone(e, g):
+            if e == 0:
+                grouped[0, g, None] = place(f"grouped0{g}", 1024)
+            nc.scalar.copy(
+                grouped[0, g, None][:, 512 * e : 512 * (e + 1)].bitcast(F32).rearrange("p (q u) -> p q u", u=2),
+                banks[0, g, e][:].rearrange("p (u q) -> p q u", u=2),
+            )
+
+        def turn(h, g):
+            banks[h, g] = psum.tile([P, 512], F32, name=f"bank{h}{g}", tag=f"bank{h}{g}")
             words = picks[h, g][:].bitcast(F32)
             for t in range(4):
-                nc.tensor.transpose(bank[:, P * t : P * (t + 1)], words[:, P * t : P * (t + 1)] if (h, g) == (1, 2) else words[:, t : 512 : 4], ident[:])
-            src = bank[:].bitcast(BF16).rearrange("p (t q e) -> p e q t", t=4, e=2)
-            grouped[h, g] = keep.tile([P, 1024], BF16, name=f"grouped{h}{g}", align_bytes=64)
-            dst = grouped[h, g][:].rearrange("p (e q t) -> p e q t", e=2, t=4)
-            if (h, g) in [(1, 2)]:
-                for e in range(2):
-                    nc.scalar.copy(dst[:, e], src[:, e])
+                if FOUR[h][g] == 4:
+                    src = words[:, P * t : P * (t + 1)]
+                elif FOUR[h][g] == 2:
+                    src = words[:, 256 * (t // 2) + t % 2 : 256 * (t // 2 + 1) : 2]
+                else:
+                    src = words[:, t : 512 : 4]
+                nc.tensor.transpose(banks[h, g][:, P * t : P * (t + 1)], src, ident[:])
+
+        def empty(h, g, e, engine):
+            src = banks[h, g][:].bitcast(BF16).rearrange("p (t q e) -> p e q t", t=4, e=2)
+            if e is None:
+                grouped[h, g, e] = place(f"grouped{h}{g}", 1024)
+                dst = grouped[h, g, e][:].rearrange("p (e q t) -> p e q t", e=2, t=4)
             else:
+                grouped[h, g, e] = place(f"grouped{h}{g}e{e}", 512)
+                dst = grouped[h, g, e][:].rearrange("p (q t) -> p q t", t=4)
+                src = src[:, e]
+            if engine == "s":
                 nc.scalar.copy(dst, src)
+            else:
+                nc.vector.tensor_copy(dst, src)
+
+        def quantise(h, g, e):
+            if (h, g) not in codes:
+                codes[h, g] = keep.tile([P, 256], U32, name=f"codes{h}{g}", align_bytes=64)
+                planes[h, g] = keep.tile([P, 256], U8, name=f"planes{h}{g}", align_bytes=64)
+            cols = slice(0, 256) if e is None else slice(P * e, P * (e + 1))
+            nc.vector.quantize_mx(out=codes[h, g][:, cols].bitcast(FP8X4), scales=planes[h, g][:, cols], in_=grouped[h, g, e][:])
 
         def multiply(h, g):
-            codes = keep.tile([P, 256], U32, name=f"codes{h}{g}", align_bytes=64)
-            planes = keep.tile([P, 256], U8, name=f"planes{h}{g}", align_bytes=64)
-            for e in range(2) if (h, g) in [(1, 2)] else [slice(0, 2)]:
-                lo, hi = (e.start, e.stop) if (h, g) not in [(1, 2)] else (e, e + 1)
-                half = slice(P * lo, P * hi)
-                nc.vector.quantize_mx(out=codes[:, half].bitcast(FP8X4), scales=planes[:, half], in_=grouped[h, g][:, 512 * lo : 512 * hi])
             for m in range(2):
+                if g == 0:
+                    acc[h, m] = psum.tile([P, 256], F32, name=f"acc{h}{m}", tag=f"acc{m}" if h == 0 else f"bank0{m}")
                 cols = slice(P * m, P * (m + 1))
                 nc.tensor.matmul_mx(
                     out=acc[h, m][:],
                     lhsT=w_codes[:, g, cols].bitcast(FP8X4),
                     lhsT_scale=w_planes[:, g, cols],
-                    rhs=codes[:].bitcast(FP8X4),
-                    rhs_scale=planes[:],
+                    rhs=codes[h, g][:].bitcast(FP8X4),
+                    rhs_scale=planes[h, g][:],
                     start=(g == 0),
                     stop=(g == PASSES - 1),
                 )
 
-        cast("v", 0, 0, 0, 576)
-        cast("v", 0, 1, 0, 576)
-        cast("v", 0, 2, 0, 256)
-        cast("s", 0, 2, 256, 384)
-        cast("s", 1, 0, 0, 576)
-        cast("s", 1, 1, 0, 192)
-        cast("s", 1, 2, 0, 256)
-
-        picks = {(0, g): gather(0, g) for g in range(PASSES)}
-        cast("v", 1, 1, 192, 576)
-        cast("v", 1, 2, 256, 384)
-        for g in range(PASSES):
-            picks[1, g] = gather(1, g)
-        for h in range(HALVES):
-            for g in range(PASSES):
-                turn_over(h, g)
-        for h in range(HALVES):
-            for g in range(PASSES):
-                multiply(h, g)
+        def finish(h):
             for m in range(2):
-                y = keep.tile([P, 256], F32, name=f"y{h}{m}")
+                if f"y{h}{m}" in PLACE:
+                    y = shared.tile([P, 256], F32, name=f"y{h}{m}", align_bytes=64, offset=PLACE[f"y{h}{m}"])
+                else:
+                    y = keep.tile([P, 256], F32, name=f"y{h}{m}")
                 nc.scalar.activation(y[:], acc[h, m][:], SILU, bias=bias[:, m : m + 1])
                 nc.sync.dma_start(out[P * m : P * (m + 1), 256 * h : 256 * (h + 1)], y[:])
+
+        gather_alone(0, 0)
+        gather_alone(1, 0)
+        cast(0, 0)
+        cast(0, 1)
+        cast(0, 2)
+        gather(0, 1)
+        gather(0, 2)
+        cast(1, 0)
+        cast(1, 1)
+        cast(1, 2)
+        turn_alone(0, 0)
+        turn_alone(1, 0)
+        empty_alone(0, 0)
+        empty_alone(1, 0)
+        gather(1, 0)
+        turn(0, 1)
+        turn(0, 2)
+        turn(1, 0)
+        empty(0, 1, None, "s")
+        empty(0, 2, None, "s")
+        empty(1, 0, None, "s")
+        quantise(0, 0, None)
+        gather(1, 1)
+        turn(1, 1)
+        empty(1, 1, None, "s")
+        quantise(0, 1, None)
+        gather(1, 2)
+        turn(1, 2)
+        quantise(0, 2, None)
+        quantise(1, 0, None)
+        empty(1, 2, 0, "s")
+        empty(1, 2, 1, "s")
+        quantise(1, 1, None)
+        quantise(1, 2, 0)
+        quantise(1, 2, 1)
+        multiply(0, 0)
+        multiply(0, 1)
+        multiply(0, 2)
+        multiply(1, 0)
+        multiply(1, 1)
+        multiply(1, 2)
+        finish(0)
+        finish(1)

@@ -18,13 +18,27 @@ MULT = mybir.AluOpType.mult
 ADD = mybir.AluOpType.add
 
 P = 128
-PASSES = K // 512
-HALVES = T // 256
-CUTS = [[0,512,1024,1536],[0,512,1024,1536]]
-CASTS = [[[["s",0,512]],[["g",0,512]],[["s",0,512]]],[[["s",0,512]],[["g",0,512]],[["g",0,192],["s",192,512]]]]
-FOUR = [[1,1,1],[4,4,4]]
-HALFTAG = [["bank00", "acc0"]]
-HOLD = 2
+PACK = 4
+K_PASS = P * PACK
+PASSES = K // K_PASS
+LAST = PASSES - 1
+HALF = 2 * P
+COLUMN = 16
+
+CUTS = [[0, 512, 1024, 1536], [0, 512, 1024, 1280, 1536]]
+SHARES = [
+    [[("scalar", 0, 512)], [("vector", 0, 512)], [("scalar", 0, 288), ("gpsimd", 288, 512)]],
+    [
+        [("scalar", 0, 320), ("gpsimd", 320, 512)],
+        [("scalar", 0, 96), ("gpsimd", 96, 512)],
+        [("scalar", 0, 256)],
+        [("gpsimd", 0, 168), ("scalar", 168, 256)],
+    ],
+]
+
+LAST_CHUNK_AT = 3072
+GROUPED_AT = {(0, 2, None): 2048, (0, 1, None): 4096, (1, LAST, 0): 9216}
+RESULT_AT = {(0, 0): 8704, (0, 1): 9728}
 
 
 def tile_picked_actorder_lin_silu_perm_l_kernel(tc, x, w_words, w_scales, b, offs, out):
@@ -34,39 +48,31 @@ def tile_picked_actorder_lin_silu_perm_l_kernel(tc, x, w_words, w_scales, b, off
         psum = ctx.enter_context(tc.psum_pool(name="psum", bufs=1))
         shared = ctx.enter_context(tc.tile_pool(name="shared", bufs=1))
 
-        offsets = keep.tile([P, K // 16], U16, name="offsets")
+        def sbuf(name, shape, dtype, offset=None):
+            if offset is None:
+                return keep.tile(shape, dtype, name=name, align_bytes=64)
+            return shared.tile(shape, dtype, name=name, align_bytes=64, offset=offset)
+
+        offsets = keep.tile([P, K // COLUMN], U16, name="offsets")
         ident = keep.tile([P, P], F32, name="ident")
-        w_codes = keep.tile([P, PASSES, N], U32, name="w_codes", align_bytes=64)
-        w_planes = keep.tile([P, PASSES, N], U8, name="w_planes", align_bytes=64)
+        w_codes = sbuf("w_codes", [P, PASSES, N], U32)
+        w_planes = sbuf("w_planes", [P, PASSES, N], U8)
         bias = keep.tile([P, 2], F32, name="bias")
-        warm = keep.tile([P, 1], F32, name="warm")
-        warm2 = keep.tile([P, 1], F32, name="warm2")
+        zero = keep.tile([P, 1], F32, name="zero")
+        unread = keep.tile([P, 1], F32, name="unread")
 
-        rows0 = keep.tile([P, 2, K], F32, name="rows0", align_bytes=64)
-        raws = {}
-        pairs = []
-        for h in range(HALVES):
-            pairs.append(keep.tile([P, 2 * K], BF16, name=f"pairs{h}", tag=f"pairs{h}", align_bytes=64))
-            for c in range(len(CUTS[h]) - 1):
-                if h == 0:
-                    raws[h, c] = rows0[:, :, CUTS[h][c] : CUTS[h][c + 1]]
-                elif (h, c) == (1, HOLD):
-                    raws[h, c] = shared.tile([P, 2, CUTS[h][c + 1] - CUTS[h][c]], F32, name=f"raw{h}_{c}", align_bytes=64, offset=3072)
-                else:
-                    raws[h, c] = keep.tile([P, 2, CUTS[h][c + 1] - CUTS[h][c]], F32, name=f"raw{h}_{c}", align_bytes=64)
+        rows = sbuf("rows", [P, 2, K], F32)
+        pairs = [sbuf(f"pairs{h}", [P, 2 * K], BF16) for h in range(2)]
+        chunks = [[rows[:, :, lo:hi] for lo, hi in zip(CUTS[0], CUTS[0][1:])], []]
+        for lo, hi in zip(CUTS[1], CUTS[1][1:]):
+            chunks[1].append(sbuf(f"chunk{lo}", [P, 2, hi - lo], F32, LAST_CHUNK_AT if hi == K else None))
 
-        def load_x(h, c):
-            nc.sync.dma_start(
-                raws[h, c][:],
-                x[256 * h : 256 * (h + 1), CUTS[h][c] : CUTS[h][c + 1]].rearrange("(e p) c -> p e c", e=2),
-            )
-
-        nc.sync.dma_start(rows0[:, 0, :], x[0:P, :])
+        nc.sync.dma_start(rows[:, 0, :], x[0:P, :])
         nc.sync.dma_start(offsets[:], offs)
-        for c in range(len(CUTS[0]) - 1):
-            nc.sync.dma_start(rows0[:, 1, CUTS[0][c] : CUTS[0][c + 1]], x[P : 2 * P, CUTS[0][c] : CUTS[0][c + 1]])
-        for c in range(len(CUTS[1]) - 1):
-            load_x(1, c)
+        for lo, hi in zip(CUTS[0], CUTS[0][1:]):
+            nc.sync.dma_start(rows[:, 1, lo:hi], x[P:HALF, lo:hi])
+        for c, (lo, hi) in enumerate(zip(CUTS[1], CUTS[1][1:])):
+            nc.sync.dma_start(chunks[1][c][:], x[HALF:T, lo:hi].rearrange("(e p) c -> p e c", e=2))
         nc.sync.dma_start(w_codes[:].bitcast(I32), w_words.rearrange("a p n r -> p a (n r)").bitcast(I32))
         nc.vector.memset(w_planes[:].bitcast(U32), 0)
         for q in range(4):
@@ -76,162 +82,139 @@ def tile_picked_actorder_lin_silu_perm_l_kernel(tc, x, w_words, w_scales, b, off
             )
         nc.sync.dma_start(bias[:], b.rearrange("(m p) o -> p (m o)", p=P))
 
-        nc.vector.memset(warm[:], 0.0)
-        nc.scalar.activation(warm2[:], warm[:], SILU)
+        nc.vector.memset(zero[:], 0.0)
+        nc.scalar.activation(unread[:], zero[:], SILU)
         make_identity(nc, ident[:])
 
-        def cast(h, c):
-            for engine, lo, hi in CASTS[h][c]:
-                src = raws[h, c][:, :, lo:hi].rearrange("p e c -> p c e")
-                dst = pairs[h][:, 2 * (CUTS[h][c] + lo) : 2 * (CUTS[h][c] + hi)].rearrange("p (c e) -> p c e", e=2)
-                if engine == "v":
-                    nc.vector.tensor_copy(dst, src)
-                elif engine == "s":
-                    nc.scalar.copy(dst, src)
-                else:
-                    nc.gpsimd.tensor_scalar(dst, src, 1.0, 0.0, MULT, ADD)
+        picked, banks, grouped, codes, planes, sums = {}, {}, {}, {}, {}, {}
 
-        PLACE = {"grouped02": 2048, "grouped01": 6144, "grouped12e0": 9216, "y00": 8704, "y01": 9728}
+        def entries(g):
+            return offsets[:, K_PASS // COLUMN * g : K_PASS // COLUMN * (g + 1)]
 
-        def place(name, cols):
-            if name in PLACE:
-                return shared.tile([P, cols], BF16, name=name, align_bytes=64, offset=PLACE[name])
-            return keep.tile([P, cols], BF16, name=name, align_bytes=64)
+        def round_into_pairs(h):
+            for c, shares in enumerate(SHARES[h]):
+                for engine, lo, hi in shares:
+                    src = chunks[h][c][:, :, lo:hi].rearrange("p e c -> p c e")
+                    dst = pairs[h][:, 2 * (CUTS[h][c] + lo) : 2 * (CUTS[h][c] + hi)].rearrange("p (c e) -> p c e", e=2)
+                    if engine == "vector":
+                        nc.vector.tensor_copy(dst, src)
+                    elif engine == "scalar":
+                        nc.scalar.copy(dst, src)
+                    else:
+                        nc.gpsimd.tensor_scalar(dst, src, 1.0, 0.0, MULT, ADD)
 
-        picks = {}
-        banks = {}
-        grouped = {}
-        codes = {}
-        planes = {}
-        acc = {}
+        def gather_alone(e):
+            picked[0, 0, e] = sbuf(f"alone{e}", [P, K_PASS], BF16)
+            nc.vector.tensor_copy(
+                picked[0, 0, e][:].rearrange("p (u q f) -> p q u f", u=2, f=2), rows[:, e, :].indirect(entries(0))
+            )
+
+        def turn_alone(e):
+            bank = psum.tile([P, 2 * P], F32, name=f"bank_alone{e}", tag=["bank00", "sum0"][e])
+            words = picked[0, 0, e][:].bitcast(F32)
+            for u in range(2):
+                nc.tensor.transpose(bank[:, P * u : P * (u + 1)], words[:, P * u : P * (u + 1)], ident[:])
+            banks[0, 0, e] = bank
+
+        def empty_alone(e):
+            nc.scalar.copy(
+                grouped[0, 0, None][:, K_PASS * e : K_PASS * (e + 1)].bitcast(F32).rearrange("p (q u) -> p q u", u=2),
+                banks[0, 0, e][:].rearrange("p (u q) -> p q u", u=2),
+            )
 
         def gather(h, g):
-            picks[h, g] = place(f"picked{h}{g}", 1024)
-            words = picks[h, g][:].bitcast(U32)
-            if FOUR[h][g] == 4:
-                words = words.rearrange("p (t q) -> p q t", t=4)
-            elif FOUR[h][g] == 2:
-                words = words.rearrange("p (u q f) -> p q u f", u=2, f=2)
-            nc.vector.tensor_copy(words, pairs[h][:].bitcast(U32).indirect(offsets[:, 32 * g : 32 * (g + 1)]))
-
-        def gather_alone(e, g):
-            picks[0, g, e] = place(f"alone{g}{e}", 512)
-            nc.vector.tensor_copy(
-                picks[0, g, e][:].rearrange("p (u q f) -> p q u f", u=2, f=2),
-                rows0[:, e, :].indirect(offsets[:, 32 * g : 32 * (g + 1)]),
-            )
-
-        def turn_alone(e, g):
-            banks[0, g, e] = psum.tile([P, 256], F32, name=f"half{g}{e}", tag=HALFTAG[g][e])
-            words = picks[0, g, e][:].bitcast(F32)
-            for u in range(2):
-                nc.tensor.transpose(banks[0, g, e][:, P * u : P * (u + 1)], words[:, P * u : P * (u + 1)], ident[:])
-
-        def empty_alone(e, g):
-            if e == 0:
-                grouped[0, g, None] = place(f"grouped0{g}", 1024)
-            nc.scalar.copy(
-                grouped[0, g, None][:, 512 * e : 512 * (e + 1)].bitcast(F32).rearrange("p (q u) -> p q u", u=2),
-                banks[0, g, e][:].rearrange("p (u q) -> p q u", u=2),
-            )
+            picked[h, g] = sbuf(f"picked{h}{g}", [P, 2 * K_PASS], BF16)
+            words = picked[h, g][:].bitcast(U32)
+            if h == 1:
+                words = words.rearrange("p (t q) -> p q t", t=PACK)
+            nc.vector.tensor_copy(words, pairs[h][:].bitcast(U32).indirect(entries(g)))
 
         def turn(h, g):
-            banks[h, g] = psum.tile([P, 512], F32, name=f"bank{h}{g}", tag=f"bank{h}{g}")
-            words = picks[h, g][:].bitcast(F32)
-            for t in range(4):
-                if FOUR[h][g] == 4:
-                    src = words[:, P * t : P * (t + 1)]
-                elif FOUR[h][g] == 2:
-                    src = words[:, 256 * (t // 2) + t % 2 : 256 * (t // 2 + 1) : 2]
-                else:
-                    src = words[:, t : 512 : 4]
+            banks[h, g] = psum.tile([P, K_PASS], F32, name=f"bank{h}{g}", tag=f"bank{h}{g}")
+            words = picked[h, g][:].bitcast(F32)
+            for t in range(PACK):
+                src = words[:, P * t : P * (t + 1)] if h == 1 else words[:, t:K_PASS:PACK]
                 nc.tensor.transpose(banks[h, g][:, P * t : P * (t + 1)], src, ident[:])
 
-        def empty(h, g, e, engine):
-            src = banks[h, g][:].bitcast(BF16).rearrange("p (t q e) -> p e q t", t=4, e=2)
+        def empty(h, g, e=None):
+            src = banks[h, g][:].bitcast(BF16).rearrange("p (t q e) -> p e q t", t=PACK, e=2)
+            width = 2 * K_PASS if e is None else K_PASS
+            grouped[h, g, e] = sbuf(f"grouped{h}{g}{e}", [P, width], BF16, GROUPED_AT.get((h, g, e)))
             if e is None:
-                grouped[h, g, e] = place(f"grouped{h}{g}", 1024)
-                dst = grouped[h, g, e][:].rearrange("p (e q t) -> p e q t", e=2, t=4)
+                nc.scalar.copy(grouped[h, g, e][:].rearrange("p (e q t) -> p e q t", e=2, t=PACK), src)
             else:
-                grouped[h, g, e] = place(f"grouped{h}{g}e{e}", 512)
-                dst = grouped[h, g, e][:].rearrange("p (q t) -> p q t", t=4)
-                src = src[:, e]
-            if engine == "s":
-                nc.scalar.copy(dst, src)
-            else:
-                nc.vector.tensor_copy(dst, src)
+                nc.scalar.copy(grouped[h, g, e][:].rearrange("p (q t) -> p q t", t=PACK), src[:, e])
 
-        def quantise(h, g, e):
-            if (h, g) not in codes:
-                codes[h, g] = keep.tile([P, 256], U32, name=f"codes{h}{g}", align_bytes=64)
-                planes[h, g] = keep.tile([P, 256], U8, name=f"planes{h}{g}", align_bytes=64)
-            cols = slice(0, 256) if e is None else slice(P * e, P * (e + 1))
-            nc.vector.quantize_mx(out=codes[h, g][:, cols].bitcast(FP8X4), scales=planes[h, g][:, cols], in_=grouped[h, g, e][:])
+        def tokens(e):
+            return slice(0, HALF) if e is None else slice(P * e, P * (e + 1))
 
-        def multiply(h, g):
+        def quantise(h, g, e=None):
+            if e != 1:
+                codes[h, g] = sbuf(f"codes{h}{g}", [P, HALF], U32)
+                planes[h, g] = sbuf(f"planes{h}{g}", [P, HALF], U8)
+            nc.vector.quantize_mx(
+                out=codes[h, g][:, tokens(e)].bitcast(FP8X4), scales=planes[h, g][:, tokens(e)], in_=grouped[h, g, e][:]
+            )
+
+        def multiply(h, g, e=None):
             for m in range(2):
                 if g == 0:
-                    acc[h, m] = psum.tile([P, 256], F32, name=f"acc{h}{m}", tag=f"acc{m}" if h == 0 else f"bank0{m}")
-                cols = slice(P * m, P * (m + 1))
+                    sums[h, m] = psum.tile([P, HALF], F32, name=f"sum{h}{m}", tag=f"sum{m}" if h == 0 else f"bank0{m}")
+                channels = slice(P * m, P * (m + 1))
                 nc.tensor.matmul_mx(
-                    out=acc[h, m][:],
-                    lhsT=w_codes[:, g, cols].bitcast(FP8X4),
-                    lhsT_scale=w_planes[:, g, cols],
-                    rhs=codes[h, g][:].bitcast(FP8X4),
-                    rhs_scale=planes[h, g][:],
+                    out=sums[h, m][:, tokens(e)],
+                    lhsT=w_codes[:, g, channels].bitcast(FP8X4),
+                    lhsT_scale=w_planes[:, g, channels],
+                    rhs=codes[h, g][:, tokens(e)].bitcast(FP8X4),
+                    rhs_scale=planes[h, g][:, tokens(e)],
                     start=(g == 0),
-                    stop=(g == PASSES - 1),
+                    stop=(g == LAST and e != 0),
                 )
 
         def finish(h):
             for m in range(2):
-                if f"y{h}{m}" in PLACE:
-                    y = shared.tile([P, 256], F32, name=f"y{h}{m}", align_bytes=64, offset=PLACE[f"y{h}{m}"])
-                else:
-                    y = keep.tile([P, 256], F32, name=f"y{h}{m}")
-                nc.scalar.activation(y[:], acc[h, m][:], SILU, bias=bias[:, m : m + 1])
-                nc.sync.dma_start(out[P * m : P * (m + 1), 256 * h : 256 * (h + 1)], y[:])
+                result = sbuf(f"result{h}{m}", [P, HALF], F32, RESULT_AT.get((h, m)))
+                for e in [0, 1] if (h, m) == (1, 1) else [None]:
+                    nc.scalar.activation(result[:, tokens(e)], sums[h, m][:, tokens(e)], SILU, bias=bias[:, m : m + 1])
+                    nc.sync.dma_start(out[P * m : P * (m + 1), HALF * h : HALF * (h + 1)][:, tokens(e)], result[:, tokens(e)])
 
-        gather_alone(0, 0)
-        gather_alone(1, 0)
-        cast(0, 0)
-        cast(0, 1)
-        cast(0, 2)
-        gather(0, 1)
-        gather(0, 2)
-        cast(1, 0)
-        cast(1, 1)
-        cast(1, 2)
-        turn_alone(0, 0)
-        turn_alone(1, 0)
-        empty_alone(0, 0)
-        empty_alone(1, 0)
+        for e in range(2):
+            gather_alone(e)
+        round_into_pairs(0)
+        for g in range(1, PASSES):
+            gather(0, g)
+        round_into_pairs(1)
+        for e in range(2):
+            turn_alone(e)
+        grouped[0, 0, None] = sbuf("grouped_alone", [P, 2 * K_PASS], BF16)
+        for e in range(2):
+            empty_alone(e)
+
         gather(1, 0)
-        turn(0, 1)
-        turn(0, 2)
-        turn(1, 0)
-        empty(0, 1, None, "s")
-        empty(0, 2, None, "s")
-        empty(1, 0, None, "s")
-        quantise(0, 0, None)
+        for h, g in [(0, 1), (0, 2), (1, 0)]:
+            turn(h, g)
+        for h, g in [(0, 1), (0, 2), (1, 0)]:
+            empty(h, g)
+        quantise(0, 0)
         gather(1, 1)
         turn(1, 1)
-        empty(1, 1, None, "s")
-        quantise(0, 1, None)
-        gather(1, 2)
-        turn(1, 2)
-        quantise(0, 2, None)
-        quantise(1, 0, None)
-        empty(1, 2, 0, "s")
-        empty(1, 2, 1, "s")
-        quantise(1, 1, None)
-        quantise(1, 2, 0)
-        quantise(1, 2, 1)
-        multiply(0, 0)
-        multiply(0, 1)
-        multiply(0, 2)
-        multiply(1, 0)
-        multiply(1, 1)
-        multiply(1, 2)
-        finish(0)
-        finish(1)
+        empty(1, 1)
+        quantise(0, 1)
+        gather(1, LAST)
+        turn(1, LAST)
+        quantise(0, LAST)
+        quantise(1, 0)
+        for e in range(2):
+            empty(1, LAST, e)
+        quantise(1, 1)
+        for e in range(2):
+            quantise(1, LAST, e)
+
+        for g in range(PASSES):
+            multiply(0, g)
+        for g in range(LAST):
+            multiply(1, g)
+        for e in range(2):
+            multiply(1, LAST, e)
+        for h in range(2):
+            finish(h)

@@ -39,6 +39,8 @@ SHARES = [
 LAST_CHUNK_AT = 3072
 GROUPED_AT = {(0, 2, None): 2048, (0, 1, None): 4096, (1, LAST, 0): 9216}
 RESULT_AT = {(0, 0): 8704, (0, 1): 9728}
+PICKED_AT = {(0, 1): 12288}
+CODES_AT = {(0, 0): 12288}
 
 
 def tile_picked_actorder_lin_silu_perm_l_kernel(tc, x, w_words, w_scales, b, offs, out):
@@ -74,9 +76,10 @@ def tile_picked_actorder_lin_silu_perm_l_kernel(tc, x, w_words, w_scales, b, off
         for c, (lo, hi) in enumerate(zip(CUTS[1], CUTS[1][1:])):
             nc.sync.dma_start(chunks[1][c][:], x[HALF:T, lo:hi].rearrange("(e p) c -> p e c", e=2))
         nc.sync.dma_start(w_codes[:].bitcast(I32), w_words.rearrange("a p n r -> p a (n r)").bitcast(I32))
+        make_identity(nc, ident[:])
         nc.vector.memset(w_planes[:].bitcast(U32), 0)
         for q in range(4):
-            nc.sync.dma_start(
+            (nc.gpsimd if q < 3 else nc.scalar).dma_start(
                 w_planes[32 * q : 32 * q + 4, :, :].bitcast(I32),
                 w_scales[:, 4 * q : 4 * q + 4, :].rearrange("a q n -> q a n").bitcast(I32),
             )
@@ -84,7 +87,6 @@ def tile_picked_actorder_lin_silu_perm_l_kernel(tc, x, w_words, w_scales, b, off
 
         nc.vector.memset(zero[:], 0.0)
         nc.scalar.activation(unread[:], zero[:], SILU)
-        make_identity(nc, ident[:])
 
         picked, banks, grouped, codes, planes, sums = {}, {}, {}, {}, {}, {}
 
@@ -123,18 +125,15 @@ def tile_picked_actorder_lin_silu_perm_l_kernel(tc, x, w_words, w_scales, b, off
             )
 
         def gather(h, g):
-            picked[h, g] = sbuf(f"picked{h}{g}", [P, 2 * K_PASS], BF16)
-            words = picked[h, g][:].bitcast(U32)
-            if h == 1:
-                words = words.rearrange("p (t q) -> p q t", t=PACK)
+            picked[h, g] = sbuf(f"picked{h}{g}", [P, 2 * K_PASS], BF16, PICKED_AT.get((h, g)))
+            words = picked[h, g][:].bitcast(U32).rearrange("p (t q) -> p q t", t=PACK)
             nc.vector.tensor_copy(words, pairs[h][:].bitcast(U32).indirect(entries(g)))
 
         def turn(h, g):
             banks[h, g] = psum.tile([P, K_PASS], F32, name=f"bank{h}{g}", tag=f"bank{h}{g}")
             words = picked[h, g][:].bitcast(F32)
             for t in range(PACK):
-                src = words[:, P * t : P * (t + 1)] if h == 1 else words[:, t:K_PASS:PACK]
-                nc.tensor.transpose(banks[h, g][:, P * t : P * (t + 1)], src, ident[:])
+                nc.tensor.transpose(banks[h, g][:, P * t : P * (t + 1)], words[:, P * t : P * (t + 1)], ident[:])
 
         def empty(h, g, e=None):
             src = banks[h, g][:].bitcast(BF16).rearrange("p (t q e) -> p e q t", t=PACK, e=2)
@@ -150,7 +149,7 @@ def tile_picked_actorder_lin_silu_perm_l_kernel(tc, x, w_words, w_scales, b, off
 
         def quantise(h, g, e=None):
             if e != 1:
-                codes[h, g] = sbuf(f"codes{h}{g}", [P, HALF], U32)
+                codes[h, g] = sbuf(f"codes{h}{g}", [P, HALF], U32, CODES_AT.get((h, g)))
                 planes[h, g] = sbuf(f"planes{h}{g}", [P, HALF], U8)
             nc.vector.quantize_mx(
                 out=codes[h, g][:, tokens(e)].bitcast(FP8X4), scales=planes[h, g][:, tokens(e)], in_=grouped[h, g, e][:]

@@ -158,24 +158,24 @@ def tile_picked_actorder_lin_silu_perm_l_kernel(tc, x, w_words, w_scales, b, off
         def multiply(h, g, e=None):
             for m in range(2):
                 if g == 0:
-                    sums[h, m] = psum.tile([P, HALF], F32, name=f"sum{h}{m}", tag=f"sum{m}" if h == 0 else f"bank0{m}")
+                    tag = f"sum{m}" if h == 0 else ["bank00", "bank01", "bank02", "bank10"][2 * e + m]
+                    sums[h, m, e] = psum.tile([P, HALF if e is None else P], F32, name=f"sum{h}{m}{e}", tag=tag)
                 channels = slice(P * m, P * (m + 1))
                 nc.tensor.matmul_mx(
-                    out=sums[h, m][:, tokens(e)],
+                    out=sums[h, m, e][:],
                     lhsT=w_codes[:, g, channels].bitcast(FP8X4),
                     lhsT_scale=w_planes[:, g, channels],
                     rhs=codes[h, g][:, tokens(e)].bitcast(FP8X4),
                     rhs_scale=planes[h, g][:, tokens(e)],
                     start=(g == 0),
-                    stop=(g == LAST and e != 0),
+                    stop=(g == LAST),
                 )
 
-        def finish(h):
+        def finish(h, e=None):
             for m in range(2):
-                result = sbuf(f"result{h}{m}", [P, HALF], F32, RESULT_AT.get((h, m)))
-                for e in [0, 1] if (h, m) == (1, 1) else [None]:
-                    nc.scalar.activation(result[:, tokens(e)], sums[h, m][:, tokens(e)], SILU, bias=bias[:, m : m + 1])
-                    nc.sync.dma_start(out[P * m : P * (m + 1), HALF * h : HALF * (h + 1)][:, tokens(e)], result[:, tokens(e)])
+                result = sbuf(f"result{h}{m}{e}", [P, HALF if e is None else P], F32, RESULT_AT.get((h, m)))
+                nc.scalar.activation(result[:], sums[h, m, e][:], SILU, bias=bias[:, m : m + 1])
+                (nc.scalar if (h, m, e) == (1, 1, 1) else nc.sync).dma_start(out[P * m : P * (m + 1), HALF * h : HALF * (h + 1)][:, tokens(e)], result[:])
 
         for e in range(2):
             gather_alone(e)
@@ -211,9 +211,9 @@ def tile_picked_actorder_lin_silu_perm_l_kernel(tc, x, w_words, w_scales, b, off
 
         for g in range(PASSES):
             multiply(0, g)
-        for g in range(LAST):
-            multiply(1, g)
+        for g in range(PASSES):
+            for e in range(2):
+                multiply(1, g, e)
+        finish(0)
         for e in range(2):
-            multiply(1, LAST, e)
-        for h in range(2):
-            finish(h)
+            finish(1, e)

@@ -155,10 +155,10 @@ def tile_picked_actorder_lin_silu_perm_l_kernel(tc, x, w_words, w_scales, b, off
                 out=codes[h, g][:, tokens(e)].bitcast(FP8X4), scales=planes[h, g][:, tokens(e)], in_=grouped[h, g, e][:]
             )
 
-        def multiply(h, g, e=None):
-            for m in range(2):
+        def multiply(h, g, e=None, tiles=range(2)):
+            for m in tiles:
                 if g == 0:
-                    tag = f"sum{m}" if h == 0 else ["bank00", "bank01", "bank02", "bank10"][2 * e + m]
+                    tag = f"sum{m}" if h == 0 else ["bank00", "bank01", "bank12", "bank02"][2 * e + m]
                     sums[h, m, e] = psum.tile([P, HALF if e is None else P], F32, name=f"sum{h}{m}{e}", tag=tag)
                 channels = slice(P * m, P * (m + 1))
                 nc.tensor.matmul_mx(
@@ -209,11 +209,14 @@ def tile_picked_actorder_lin_silu_perm_l_kernel(tc, x, w_words, w_scales, b, off
         for e in range(2):
             quantise(1, LAST, e)
 
+        for m in range(2):
+            for g in range(PASSES):
+                multiply(0, g, None, [m])
         for g in range(PASSES):
-            multiply(0, g)
-        for g in range(PASSES):
-            for e in range(2):
-                multiply(1, g, e)
+            multiply(1, g, 0)
         finish(0)
+        for m in range(2):
+            for g in range(PASSES):
+                multiply(1, g, 1, [m])
         for e in range(2):
             finish(1, e)

@@ -14,8 +14,7 @@ U16 = mybir.dt.uint16
 U8 = mybir.dt.uint8
 FP8X4 = mybir.dt.float8_e4m3fn_x4
 SILU = mybir.ActivationFunctionType.Silu
-MULT = mybir.AluOpType.mult
-ADD = mybir.AluOpType.add
+COPY = mybir.ActivationFunctionType.Copy
 
 P = 128
 PACK = 4
@@ -24,23 +23,7 @@ PASSES = K // K_PASS
 LAST = PASSES - 1
 HALF = 2 * P
 COLUMN = 16
-
-CUTS = [[0, 512, 1024, 1536], [0, 512, 1024, 1280, 1536]]
-SHARES = [
-    [[("scalar", 0, 512)], [("vector", 0, 512)], [("scalar", 0, 288), ("gpsimd", 288, 512)]],
-    [
-        [("scalar", 0, 320), ("gpsimd", 320, 512)],
-        [("scalar", 0, 96), ("gpsimd", 96, 512)],
-        [("scalar", 0, 256)],
-        [("gpsimd", 0, 168), ("scalar", 168, 256)],
-    ],
-]
-
-LAST_CHUNK_AT = 3072
-GROUPED_AT = {(0, 2, None): 2048, (0, 1, None): 4096, (1, LAST, 0): 9216}
-RESULT_AT = {(0, 0): 8704, (0, 1): 9728}
-PICKED_AT = {(0, 1): 12288}
-CODES_AT = {(0, 0): 12288}
+SPLIT = 256
 
 
 def tile_picked_actorder_lin_silu_perm_l_kernel(tc, x, w_words, w_scales, b, offs, out):
@@ -48,12 +31,9 @@ def tile_picked_actorder_lin_silu_perm_l_kernel(tc, x, w_words, w_scales, b, off
     with ExitStack() as ctx:
         keep = ctx.enter_context(tc.tile_pool(name="keep", bufs=1))
         psum = ctx.enter_context(tc.psum_pool(name="psum", bufs=1))
-        shared = ctx.enter_context(tc.tile_pool(name="shared", bufs=1))
 
-        def sbuf(name, shape, dtype, offset=None):
-            if offset is None:
-                return keep.tile(shape, dtype, name=name, align_bytes=64)
-            return shared.tile(shape, dtype, name=name, align_bytes=64, offset=offset)
+        def sbuf(name, shape, dtype):
+            return keep.tile(shape, dtype, name=name, align_bytes=64)
 
         offsets = keep.tile([P, K // COLUMN], U16, name="offsets")
         ident = keep.tile([P, P], F32, name="ident")
@@ -62,161 +42,125 @@ def tile_picked_actorder_lin_silu_perm_l_kernel(tc, x, w_words, w_scales, b, off
         bias = keep.tile([P, 2], F32, name="bias")
         zero = keep.tile([P, 1], F32, name="zero")
         unread = keep.tile([P, 1], F32, name="unread")
+        rows = [sbuf(f"rows{blk}", [P, K], F32) for blk in range(4)]
 
-        rows = sbuf("rows", [P, 2, K], F32)
-        pairs = [sbuf(f"pairs{h}", [P, 2 * K], BF16) for h in range(2)]
-        chunks = [[rows[:, :, lo:hi] for lo, hi in zip(CUTS[0], CUTS[0][1:])], []]
-        for lo, hi in zip(CUTS[1], CUTS[1][1:]):
-            chunks[1].append(sbuf(f"chunk{lo}", [P, 2, hi - lo], F32, LAST_CHUNK_AT if hi == K else None))
+        def load_rows(blk):
+            nc.sync.dma_start(rows[blk][:], x[P * blk : P * (blk + 1), :])
 
-        nc.sync.dma_start(rows[:, 0, :], x[0:P, :])
+        load_rows(0)
         nc.sync.dma_start(offsets[:], offs)
-        for lo, hi in zip(CUTS[0], CUTS[0][1:]):
-            nc.sync.dma_start(rows[:, 1, lo:hi], x[P:HALF, lo:hi])
-        for c, (lo, hi) in enumerate(zip(CUTS[1], CUTS[1][1:])):
-            nc.sync.dma_start(chunks[1][c][:], x[HALF:T, lo:hi].rearrange("(e p) c -> p e c", e=2))
+        load_rows(1)
         nc.sync.dma_start(w_codes[:].bitcast(I32), w_words.rearrange("a p n r -> p a (n r)").bitcast(I32))
+        load_rows(2)
+        load_rows(3)
+        nc.sync.dma_start(bias[:], b.rearrange("(m p) o -> p (m o)", p=P))
         make_identity(nc, ident[:])
         nc.vector.memset(w_planes[:].bitcast(U32), 0)
         for q in range(4):
-            (nc.gpsimd if q < 3 else nc.scalar).dma_start(
+            nc.gpsimd.dma_start(
                 w_planes[32 * q : 32 * q + 4, :, :].bitcast(I32),
                 w_scales[:, 4 * q : 4 * q + 4, :].rearrange("a q n -> q a n").bitcast(I32),
             )
-        nc.sync.dma_start(bias[:], b.rearrange("(m p) o -> p (m o)", p=P))
 
         nc.vector.memset(zero[:], 0.0)
         nc.scalar.activation(unread[:], zero[:], SILU)
 
         picked, banks, grouped, codes, planes, sums = {}, {}, {}, {}, {}, {}
 
-        def entries(g):
-            return offsets[:, K_PASS // COLUMN * g : K_PASS // COLUMN * (g + 1)]
-
-        def round_into_pairs(h):
-            for c, shares in enumerate(SHARES[h]):
-                for engine, lo, hi in shares:
-                    src = chunks[h][c][:, :, lo:hi].rearrange("p e c -> p c e")
-                    dst = pairs[h][:, 2 * (CUTS[h][c] + lo) : 2 * (CUTS[h][c] + hi)].rearrange("p (c e) -> p c e", e=2)
-                    if engine == "vector":
-                        nc.vector.tensor_copy(dst, src)
-                    elif engine == "scalar":
-                        nc.scalar.copy(dst, src)
-                    else:
-                        nc.gpsimd.tensor_scalar(dst, src, 1.0, 0.0, MULT, ADD)
-
-        def gather_alone(e):
-            picked[0, 0, e] = sbuf(f"alone{e}", [P, K_PASS], BF16)
-            nc.vector.tensor_copy(
-                picked[0, 0, e][:].rearrange("p (u q f) -> p q u f", u=2, f=2), rows[:, e, :].indirect(entries(0))
-            )
-
-        def turn_alone(e):
-            bank = psum.tile([P, 2 * P], F32, name=f"bank_alone{e}", tag=["bank00", "sum0"][e])
-            words = picked[0, 0, e][:].bitcast(F32)
-            for u in range(2):
-                nc.tensor.transpose(bank[:, P * u : P * (u + 1)], words[:, P * u : P * (u + 1)], ident[:])
-            banks[0, 0, e] = bank
-
-        def empty_alone(e):
-            nc.scalar.copy(
-                grouped[0, 0, None][:, K_PASS * e : K_PASS * (e + 1)].bitcast(F32).rearrange("p (q u) -> p q u", u=2),
-                banks[0, 0, e][:].rearrange("p (u q) -> p q u", u=2),
-            )
-
-        def gather(h, g):
-            picked[h, g] = sbuf(f"picked{h}{g}", [P, 2 * K_PASS], BF16, PICKED_AT.get((h, g)))
-            words = picked[h, g][:].bitcast(U32).rearrange("p (t q) -> p q t", t=PACK)
-            nc.vector.tensor_copy(words, pairs[h][:].bitcast(U32).indirect(entries(g)))
-
-        def turn(h, g):
-            banks[h, g] = psum.tile([P, K_PASS], F32, name=f"bank{h}{g}", tag=f"bank{h}{g}")
-            words = picked[h, g][:].bitcast(F32)
-            for t in range(PACK):
-                nc.tensor.transpose(banks[h, g][:, P * t : P * (t + 1)], words[:, P * t : P * (t + 1)], ident[:])
-
-        def empty(h, g, e=None):
-            src = banks[h, g][:].bitcast(BF16).rearrange("p (t q e) -> p e q t", t=PACK, e=2)
-            width = 2 * K_PASS if e is None else K_PASS
-            grouped[h, g, e] = sbuf(f"grouped{h}{g}{e}", [P, width], BF16, GROUPED_AT.get((h, g, e)))
-            if e is None:
-                nc.scalar.copy(grouped[h, g, e][:].rearrange("p (e q t) -> p e q t", e=2, t=PACK), src)
+        def gather(engine, blk, g, lo, hi):
+            window = rows[blk][:].indirect(offsets[:, (K_PASS * g + lo) // COLUMN : (K_PASS * g + hi) // COLUMN])
+            if engine == "vector":
+                nc.vector.tensor_copy(picked[blk, g][:, lo:hi], window)
             else:
-                nc.scalar.copy(grouped[h, g, e][:].rearrange("p (q t) -> p q t", t=PACK), src[:, e])
+                nc.scalar.activation(picked[blk, g][:, lo:hi], window, COPY)
 
-        def tokens(e):
-            return slice(0, HALF) if e is None else slice(P * e, P * (e + 1))
+        def gather_block(blk):
+            for g in range(PASSES):
+                picked[blk, g] = sbuf(f"picked{blk}{g}", [P, K_PASS], BF16)
+            gather("vector", blk, 0, 0, K_PASS)
+            gather("scalar", blk, 1, 0, K_PASS)
+            gather("vector", blk, LAST, 0, SPLIT)
+            gather("scalar", blk, LAST, SPLIT, K_PASS)
 
-        def quantise(h, g, e=None):
-            if e != 1:
-                codes[h, g] = sbuf(f"codes{h}{g}", [P, HALF], U32, CODES_AT.get((h, g)))
-                planes[h, g] = sbuf(f"planes{h}{g}", [P, HALF], U8)
-            nc.vector.quantize_mx(
-                out=codes[h, g][:, tokens(e)].bitcast(FP8X4), scales=planes[h, g][:, tokens(e)], in_=grouped[h, g, e][:]
+        def turn(blk, g, bank, at):
+            words = picked[blk, g][:].bitcast(F32)
+            for u in range(2):
+                nc.tensor.transpose(bank[:, at + P * u : at + P * (u + 1)], words[:, u : 2 * P : 2], ident[:])
+
+        def empty(engine, key, blocks):
+            grouped[key] = sbuf(f"grouped{key}", [P, blocks * K_PASS], BF16)
+            dst = grouped[key][:].bitcast(F32).rearrange("p (e q u) -> p e q u", e=blocks, u=2)
+            src = banks[key][:].rearrange("p (e u q) -> p e q u", e=blocks, u=2)
+            if engine == "vector":
+                nc.vector.tensor_copy(dst, src)
+            else:
+                nc.scalar.copy(dst, src)
+
+        def quantise(key, blocks):
+            codes[key] = sbuf(f"codes{key}", [P, blocks * P], U32)
+            planes[key] = sbuf(f"planes{key}", [P, blocks * P], U8)
+            nc.vector.quantize_mx(out=codes[key][:].bitcast(FP8X4), scales=planes[key][:], in_=grouped[key][:])
+
+        def multiply(total, m, g, key, columns):
+            channels = slice(P * m, P * (m + 1))
+            nc.tensor.matmul_mx(
+                out=total[:],
+                lhsT=w_codes[:, g, channels].bitcast(FP8X4),
+                lhsT_scale=w_planes[:, g, channels],
+                rhs=codes[key][:, columns].bitcast(FP8X4),
+                rhs_scale=planes[key][:, columns],
+                start=(g == 0),
+                stop=(g == LAST),
             )
 
-        def multiply(h, g, e=None, tiles=range(2)):
-            for m in tiles:
-                if g == 0:
-                    tag = f"sum{m}" if h == 0 else ["bank00", "bank01", "bank12", "bank02"][2 * e + m]
-                    sums[h, m, e] = psum.tile([P, HALF if e is None else P], F32, name=f"sum{h}{m}{e}", tag=tag)
-                channels = slice(P * m, P * (m + 1))
-                nc.tensor.matmul_mx(
-                    out=sums[h, m, e][:],
-                    lhsT=w_codes[:, g, channels].bitcast(FP8X4),
-                    lhsT_scale=w_planes[:, g, channels],
-                    rhs=codes[h, g][:, tokens(e)].bitcast(FP8X4),
-                    rhs_scale=planes[h, g][:, tokens(e)],
-                    start=(g == 0),
-                    stop=(g == LAST),
-                )
+        def finish(total, m, first, width, queue):
+            result = sbuf(f"result{m}_{first}", [P, width], F32)
+            nc.scalar.activation(result[:], total[:], SILU, bias=bias[:, m : m + 1])
+            queue.dma_start(out[P * m : P * (m + 1), first : first + width], result[:])
 
-        def finish(h, e=None):
-            for m in range(2):
-                result = sbuf(f"result{h}{m}{e}", [P, HALF if e is None else P], F32, RESULT_AT.get((h, m)))
-                nc.scalar.activation(result[:], sums[h, m, e][:], SILU, bias=bias[:, m : m + 1])
-                (nc.scalar if (h, m, e) == (1, 1, 1) else nc.sync).dma_start(out[P * m : P * (m + 1), HALF * h : HALF * (h + 1)][:, tokens(e)], result[:])
-
-        for e in range(2):
-            gather_alone(e)
-        round_into_pairs(0)
-        for g in range(1, PASSES):
-            gather(0, g)
-        round_into_pairs(1)
-        for e in range(2):
-            turn_alone(e)
-        grouped[0, 0, None] = sbuf("grouped_alone", [P, 2 * K_PASS], BF16)
-        for e in range(2):
-            empty_alone(e)
-
-        gather(1, 0)
-        for h, g in [(0, 1), (0, 2), (1, 0)]:
-            turn(h, g)
-        for h, g in [(0, 1), (0, 2), (1, 0)]:
-            empty(h, g)
-        quantise(0, 0)
-        gather(1, 1)
-        turn(1, 1)
-        empty(1, 1)
-        quantise(0, 1)
-        gather(1, LAST)
-        turn(1, LAST)
-        quantise(0, LAST)
-        quantise(1, 0)
-        for e in range(2):
-            empty(1, LAST, e)
-        quantise(1, 1)
-        for e in range(2):
-            quantise(1, LAST, e)
-
-        for m in range(2):
-            for g in range(PASSES):
-                multiply(0, g, None, [m])
         for g in range(PASSES):
-            multiply(1, g, 0)
-        finish(0)
-        for m in range(2):
+            banks[f"0{g}"] = psum.tile([P, 2 * HALF], F32, name=f"bank0{g}", tag=f"t{g}")
+        for blk in range(2):
+            gather_block(blk)
             for g in range(PASSES):
-                multiply(1, g, 1, [m])
+                turn(blk, g, banks[f"0{g}"], HALF * blk)
+        empty("vector", "00", 2)
+        empty("scalar", "01", 2)
+        empty("scalar", "02", 2)
+        for g in [1, 0, 2]:
+            quantise(f"0{g}", 2)
+        for m in range(2):
+            sums[0, m] = psum.tile([P, HALF], F32, name=f"sum0{m}", tag=f"s{m}")
+            for g in range(PASSES):
+                multiply(sums[0, m], m, g, f"0{g}", slice(0, HALF))
+
+        for g in range(2):
+            banks[f"1{g}"] = psum.tile([P, 2 * HALF], F32, name=f"bank1{g}", tag=f"t{3 + g}")
+        banks["2b2"] = psum.tile([P, HALF], F32, name="bank2b2", tag="t5")
+        banks["2b3"] = psum.tile([P, HALF], F32, name="bank2b3", tag="t0")
+        gather_block(2)
+        for g in range(2):
+            turn(2, g, banks[f"1{g}"], 0)
+        turn(2, LAST, banks["2b2"], 0)
+        for m in range(2):
+            finish(sums[0, m], m, 0, HALF, nc.sync)
+        empty("scalar", "2b2", 1)
+        quantise("2b2", 1)
+        gather_block(3)
+        for g in range(2):
+            turn(3, g, banks[f"1{g}"], HALF)
+        turn(3, LAST, banks["2b3"], 0)
+        empty("vector", "10", 2)
+        empty("scalar", "11", 2)
+        empty("scalar", "2b3", 1)
+        for key, blocks in [("11", 2), ("10", 2), ("2b3", 1)]:
+            quantise(key, blocks)
         for e in range(2):
-            finish(1, e)
+            for m in range(2):
+                sums[2 + e, m] = psum.tile([P, P], F32, name=f"sum{2 + e}{m}", tag=f"t{1 + 2 * e + m}")
+                for g in range(2):
+                    multiply(sums[2 + e, m], m, g, f"1{g}", slice(P * e, P * (e + 1)))
+                multiply(sums[2 + e, m], m, LAST, f"2b{2 + e}", slice(0, P))
+        for e in range(2):
+            for m in range(2):
+                finish(sums[2 + e, m], m, HALF + P * e, P, nc.scalar if (e, m) == (1, 1) else nc.sync)

@@ -23,7 +23,22 @@ PASSES = K // K_PASS
 LAST = PASSES - 1
 HALF = 2 * P
 COLUMN = 16
-SPLIT = 256
+BLOCKS = T // P
+SHARES = [
+    [("vector", 0, 0, 512), ("scalar", 1, 0, 512), ("vector", 2, 0, 256), ("scalar", 2, 256, 512)],
+    [("vector", 0, 0, 512), ("scalar", 2, 0, 512), ("vector", 1, 0, 512)],
+    [("vector", 0, 0, 512), ("scalar", 2, 0, 512), ("vector", 1, 0, 384), ("scalar", 1, 384, 512)],
+    [("scalar", 0, 0, 512), ("vector", 1, 0, 512), ("vector", 2, 0, 128), ("scalar", 2, 128, 512)],
+]
+SHARED_AT = {
+    "staged0": 0,
+    "grouped00": 0,
+    "landed0": 3072,
+    "grouped10": 3072,
+    "landed1": 8192 - 64,
+    "grouped20": 8192 - 2048,
+    "grouped22": 8192,
+}
 
 
 def tile_picked_actorder_lin_silu_perm_l_kernel(tc, x, w_words, w_scales, b, offs, out):
@@ -31,18 +46,23 @@ def tile_picked_actorder_lin_silu_perm_l_kernel(tc, x, w_words, w_scales, b, off
     with ExitStack() as ctx:
         keep = ctx.enter_context(tc.tile_pool(name="keep", bufs=1))
         psum = ctx.enter_context(tc.psum_pool(name="psum", bufs=1))
+        shared = ctx.enter_context(tc.tile_pool(name="shared", bufs=1))
 
         def sbuf(name, shape, dtype):
+            if name in SHARED_AT:
+                return shared.tile(shape, dtype, name=name, align_bytes=64, offset=SHARED_AT[name])
             return keep.tile(shape, dtype, name=name, align_bytes=64)
 
         offsets = keep.tile([P, K // COLUMN], U16, name="offsets")
         ident = keep.tile([P, P], F32, name="ident")
         w_codes = sbuf("w_codes", [P, PASSES, N], U32)
         w_planes = sbuf("w_planes", [P, PASSES, N], U8)
-        bias = keep.tile([P, 2], F32, name="bias")
+        staged = [sbuf(f"staged{q}", [P, PASSES, N], U8) for q in range(4)]
+        bias = [sbuf(f"bias{m}", [P, 1], F32) for m in range(2)]
+        landed = [sbuf(f"landed{m}", [P, 32], F32) for m in range(2)]
         zero = keep.tile([P, 1], F32, name="zero")
         unread = keep.tile([P, 1], F32, name="unread")
-        rows = [sbuf(f"rows{blk}", [P, K], F32) for blk in range(4)]
+        rows = [sbuf(f"rows{blk}", [P, K], F32) for blk in range(BLOCKS)]
 
         def load_rows(blk):
             nc.sync.dma_start(rows[blk][:], x[P * blk : P * (blk + 1), :])
@@ -50,117 +70,132 @@ def tile_picked_actorder_lin_silu_perm_l_kernel(tc, x, w_words, w_scales, b, off
         load_rows(0)
         nc.sync.dma_start(offsets[:], offs)
         load_rows(1)
-        nc.sync.dma_start(w_codes[:].bitcast(I32), w_words.rearrange("a p n r -> p a (n r)").bitcast(I32))
-        load_rows(2)
-        load_rows(3)
-        nc.sync.dma_start(bias[:], b.rearrange("(m p) o -> p (m o)", p=P))
-        make_identity(nc, ident[:])
-        nc.vector.memset(w_planes[:].bitcast(U32), 0)
         for q in range(4):
-            nc.gpsimd.dma_start(
-                w_planes[32 * q : 32 * q + 4, :, :].bitcast(I32),
+            nc.sync.dma_start(
+                staged[q][32 * q : 32 * q + 4, :, :].bitcast(I32),
                 w_scales[:, 4 * q : 4 * q + 4, :].rearrange("a q n -> q a n").bitcast(I32),
             )
+        nc.sync.dma_start(w_codes[:].bitcast(I32), w_words.rearrange("a p n r -> p a (n r)").bitcast(I32))
+        for m in range(2):
+            load_rows(2 + m)
+            nc.sync.dma_start(landed[m][:, 0:1], b[P * m : P * (m + 1), :])
+        make_identity(nc, ident[:])
+        nc.gpsimd.memset(w_planes[:].bitcast(U32), 0)
+        for q in range(4):
+            live = slice(32 * q, 32 * q + 4)
+            nc.gpsimd.tensor_copy(w_planes[live, :, :].bitcast(I32), staged[q][live, :, :].bitcast(I32))
+        for m in range(2):
+            nc.gpsimd.tensor_copy(bias[m][:], landed[m][:, 0:1])
 
         nc.vector.memset(zero[:], 0.0)
         nc.scalar.activation(unread[:], zero[:], SILU)
 
         picked, banks, grouped, codes, planes, sums = {}, {}, {}, {}, {}, {}
 
-        def gather(engine, blk, g, lo, hi):
-            window = rows[blk][:].indirect(offsets[:, (K_PASS * g + lo) // COLUMN : (K_PASS * g + hi) // COLUMN])
-            if engine == "vector":
-                nc.vector.tensor_copy(picked[blk, g][:, lo:hi], window)
-            else:
-                nc.scalar.activation(picked[blk, g][:, lo:hi], window, COPY)
-
-        def gather_block(blk):
+        def gather(blk):
             for g in range(PASSES):
                 picked[blk, g] = sbuf(f"picked{blk}{g}", [P, K_PASS], BF16)
-            gather("vector", blk, 0, 0, K_PASS)
-            gather("scalar", blk, 1, 0, K_PASS)
-            gather("vector", blk, LAST, 0, SPLIT)
-            gather("scalar", blk, LAST, SPLIT, K_PASS)
+            for engine, g, lo, hi in SHARES[blk]:
+                window = rows[blk][:].indirect(offsets[:, (K_PASS * g + lo) // COLUMN : (K_PASS * g + hi) // COLUMN])
+                if engine == "vector":
+                    nc.vector.tensor_copy(picked[blk, g][:, lo:hi], window)
+                else:
+                    nc.scalar.activation(picked[blk, g][:, lo:hi], window, COPY)
 
-        def turn(blk, g, bank, at):
-            words = picked[blk, g][:].bitcast(F32)
-            for u in range(2):
-                nc.tensor.transpose(bank[:, at + P * u : at + P * (u + 1)], words[:, u : 2 * P : 2], ident[:])
+        def turn(blk, passes, tag):
+            bank = psum.tile([P, HALF * len(passes)], F32, name=f"bank{blk}{passes[0]}", tag=tag)
+            banks[blk, passes] = bank
+            for i, g in enumerate(passes):
+                words = picked[blk, g][:].bitcast(F32)
+                for u in range(2):
+                    at = HALF * i + P * u
+                    nc.tensor.transpose(bank[:, at : at + P], words[:, u:HALF:2], ident[:])
 
-        def empty(engine, key, blocks):
-            grouped[key] = sbuf(f"grouped{key}", [P, blocks * K_PASS], BF16)
-            dst = grouped[key][:].bitcast(F32).rearrange("p (e q u) -> p e q u", e=blocks, u=2)
-            src = banks[key][:].rearrange("p (e u q) -> p e q u", e=blocks, u=2)
+        def group(blk, passes):
+            grouped[blk, passes] = sbuf(f"grouped{blk}{passes[0]}", [P, K_PASS * len(passes)], BF16)
+
+        def empty(engine, blk, passes, into):
+            first = into.index(passes[0])
+            dst = grouped[blk, into][:, K_PASS * first : K_PASS * (first + len(passes))]
+            dst = dst.bitcast(F32).rearrange("p (g q u) -> p g q u", g=len(passes), u=2)
+            src = banks[blk, passes][:].rearrange("p (g u q) -> p g q u", g=len(passes), u=2)
             if engine == "vector":
                 nc.vector.tensor_copy(dst, src)
             else:
                 nc.scalar.copy(dst, src)
 
-        def quantise(key, blocks):
-            codes[key] = sbuf(f"codes{key}", [P, blocks * P], U32)
-            planes[key] = sbuf(f"planes{key}", [P, blocks * P], U8)
-            nc.vector.quantize_mx(out=codes[key][:].bitcast(FP8X4), scales=planes[key][:], in_=grouped[key][:])
+        def quantise(blk, passes):
+            made = sbuf(f"codes{blk}{passes[0]}", [P, P * len(passes)], U32)
+            scales = sbuf(f"planes{blk}{passes[0]}", [P, P * len(passes)], U8)
+            nc.vector.quantize_mx(out=made[:].bitcast(FP8X4), scales=scales[:], in_=grouped[blk, passes][:])
+            for i, g in enumerate(passes):
+                codes[blk, g] = made[:, P * i : P * (i + 1)]
+                planes[blk, g] = scales[:, P * i : P * (i + 1)]
 
-        def multiply(total, m, g, key, columns):
+        def multiply(blk, m, order, tag):
+            sums[blk, m] = psum.tile([P, P], F32, name=f"sum{blk}{m}", tag=tag)
             channels = slice(P * m, P * (m + 1))
-            nc.tensor.matmul_mx(
-                out=total[:],
-                lhsT=w_codes[:, g, channels].bitcast(FP8X4),
-                lhsT_scale=w_planes[:, g, channels],
-                rhs=codes[key][:, columns].bitcast(FP8X4),
-                rhs_scale=planes[key][:, columns],
-                start=(g == 0),
-                stop=(g == LAST),
-            )
+            for g in order:
+                nc.tensor.matmul_mx(
+                    out=sums[blk, m][:],
+                    lhsT=w_codes[:, g, channels].bitcast(FP8X4),
+                    lhsT_scale=w_planes[:, g, channels],
+                    rhs=codes[blk, g].bitcast(FP8X4),
+                    rhs_scale=planes[blk, g],
+                    start=(g == order[0]),
+                    stop=(g == order[-1]),
+                )
 
-        def finish(total, m, first, width, queue):
-            result = sbuf(f"result{m}_{first}", [P, width], F32)
-            nc.scalar.activation(result[:], total[:], SILU, bias=bias[:, m : m + 1])
-            queue.dma_start(out[P * m : P * (m + 1), first : first + width], result[:])
+        def finish(blk, m, queue):
+            result = sbuf(f"result{blk}{m}", [P, P], F32)
+            nc.scalar.activation(result[:], sums[blk, m][:], SILU, bias=bias[m][:])
+            queue.dma_start(out[P * m : P * (m + 1), P * blk : P * (blk + 1)], result[:])
 
-        for g in range(PASSES):
-            banks[f"0{g}"] = psum.tile([P, 2 * HALF], F32, name=f"bank0{g}", tag=f"t{g}")
-        for blk in range(2):
-            gather_block(blk)
-            for g in range(PASSES):
-                turn(blk, g, banks[f"0{g}"], HALF * blk)
-        empty("vector", "00", 2)
-        empty("scalar", "01", 2)
-        empty("scalar", "02", 2)
-        for g in [1, 0, 2]:
-            quantise(f"0{g}", 2)
+        every = (0, 1, 2)
+
+        def empty_both(blk):
+            group(blk, every)
+            empty("scalar", blk, (0, 1), every)
+            empty("scalar", blk, (2,), every)
+            quantise(blk, every)
+
+        gather(0)
+        turn(0, (0, 1), "t0")
+        turn(0, (2,), "t1")
+        gather(1)
+        turn(1, (2,), "t3")
+        turn(1, (0, 1), "t2")
+        empty_both(0)
         for m in range(2):
-            sums[0, m] = psum.tile([P, HALF], F32, name=f"sum0{m}", tag=f"s{m}")
-            for g in range(PASSES):
-                multiply(sums[0, m], m, g, f"0{g}", slice(0, HALF))
-
-        for g in range(2):
-            banks[f"1{g}"] = psum.tile([P, 2 * HALF], F32, name=f"bank1{g}", tag=f"t{3 + g}")
-        banks["2b2"] = psum.tile([P, HALF], F32, name="bank2b2", tag="t5")
-        banks["2b3"] = psum.tile([P, HALF], F32, name="bank2b3", tag="t0")
-        gather_block(2)
-        for g in range(2):
-            turn(2, g, banks[f"1{g}"], 0)
-        turn(2, LAST, banks["2b2"], 0)
+            multiply(0, m, every, f"s{m}")
+        gather(2)
+        turn(2, (2,), "t1")
+        turn(2, (0, 1), "t0")
+        empty_both(1)
         for m in range(2):
-            finish(sums[0, m], m, 0, HALF, nc.sync)
-        empty("scalar", "2b2", 1)
-        quantise("2b2", 1)
-        gather_block(3)
-        for g in range(2):
-            turn(3, g, banks[f"1{g}"], HALF)
-        turn(3, LAST, banks["2b3"], 0)
-        empty("vector", "10", 2)
-        empty("scalar", "11", 2)
-        empty("scalar", "2b3", 1)
-        for key, blocks in [("11", 2), ("10", 2), ("2b3", 1)]:
-            quantise(key, blocks)
-        for e in range(2):
+            multiply(1, m, every, f"s{2 + m}")
+        gather(3)
+        turn(3, (0,), "t2")
+        turn(3, (1,), "t3")
+        group(2, (2,))
+        empty("scalar", 2, (2,), (2,))
+        group(2, (0, 1))
+        empty("vector", 2, (0, 1), (0, 1))
+        turn(3, (2,), "t1")
+        quantise(2, (2,))
+        quantise(2, (0, 1))
+        for m in range(2):
+            finish(0, m, nc.sync)
+        for g in every:
+            group(3, (g,))
+            empty("scalar", 3, (g,), (g,))
+            quantise(3, (g,))
+        for m in range(2):
+            multiply(2, m, (2, 0, 1), f"s{m}")
+        for m in range(2):
+            finish(1, m, nc.sync)
+        for m in range(2):
+            multiply(3, m, every, ["t0", "t2"][m])
+        for blk in (2, 3):
             for m in range(2):
-                sums[2 + e, m] = psum.tile([P, P], F32, name=f"sum{2 + e}{m}", tag=f"t{1 + 2 * e + m}")
-                for g in range(2):
-                    multiply(sums[2 + e, m], m, g, f"1{g}", slice(P * e, P * (e + 1)))
-                multiply(sums[2 + e, m], m, LAST, f"2b{2 + e}", slice(0, P))
-        for e in range(2):
-            for m in range(2):
-                finish(sums[2 + e, m], m, HALF + P * e, P, nc.scalar if (e, m) == (1, 1) else nc.sync)
+                finish(blk, m, nc.scalar if (blk, m) == (3, 1) else nc.sync)

@@ -28,7 +28,7 @@ SHARES = [
     [("vector", 0, 0, 512), ("scalar", 1, 0, 512), ("vector", 2, 0, 256), ("scalar", 2, 256, 512)],
     [("vector", 0, 0, 512), ("scalar", 2, 0, 512), ("vector", 1, 0, 512)],
     [("vector", 0, 0, 512), ("scalar", 2, 0, 512), ("vector", 1, 0, 384), ("scalar", 1, 384, 512)],
-    [("scalar", 0, 0, 512), ("vector", 1, 0, 512), ("vector", 2, 0, 128), ("scalar", 2, 128, 512)],
+    [("scalar", 0, 0, 512), ("vector", 1, 0, 320), ("scalar", 1, 320, 512), ("vector", 2, 0, 256), ("scalar", 2, 256, 512)],
 ]
 SHARED_AT = {
     "staged0": 0,
@@ -38,6 +38,9 @@ SHARED_AT = {
     "landed1": 8192 - 64,
     "grouped20": 8192 - 2048,
     "grouped22": 8192,
+    "picked30": 9216,
+    "result00": 9216,
+    "result10": 9216 + 512,
 }
 
 
@@ -55,7 +58,9 @@ def tile_picked_actorder_lin_silu_perm_l_kernel(tc, x, w_words, w_scales, b, off
 
         offsets = keep.tile([P, K // COLUMN], U16, name="offsets")
         ident = keep.tile([P, P], F32, name="ident")
-        w_codes = sbuf("w_codes", [P, PASSES, N], U32)
+        w_early = sbuf("w_early", [P, LAST, N], U32)
+        w_late = sbuf("w_late", [P, N], U32)
+        w_codes = [w_early[:, 0, :], w_early[:, 1, :], w_late[:]]
         w_planes = sbuf("w_planes", [P, PASSES, N], U8)
         staged = [sbuf(f"staged{q}", [P, PASSES, N], U8) for q in range(4)]
         bias = [sbuf(f"bias{m}", [P, 1], F32) for m in range(2)]
@@ -75,10 +80,13 @@ def tile_picked_actorder_lin_silu_perm_l_kernel(tc, x, w_words, w_scales, b, off
                 staged[q][32 * q : 32 * q + 4, :, :].bitcast(I32),
                 w_scales[:, 4 * q : 4 * q + 4, :].rearrange("a q n -> q a n").bitcast(I32),
             )
-        nc.sync.dma_start(w_codes[:].bitcast(I32), w_words.rearrange("a p n r -> p a (n r)").bitcast(I32))
-        for m in range(2):
-            load_rows(2 + m)
-            nc.sync.dma_start(landed[m][:, 0:1], b[P * m : P * (m + 1), :])
+        words_of_w = w_words.rearrange("a p n r -> p a (n r)").bitcast(I32)
+        nc.sync.dma_start(w_early[:].bitcast(I32), words_of_w[:, 0:LAST, :])
+        load_rows(2)
+        nc.sync.dma_start(landed[0][:, 0:1], b[0:P, :])
+        nc.sync.dma_start(w_late[:].bitcast(I32), words_of_w[:, LAST, :])
+        load_rows(3)
+        nc.sync.dma_start(landed[1][:, 0:1], b[P:N, :])
         make_identity(nc, ident[:])
         nc.gpsimd.memset(w_planes[:].bitcast(U32), 0)
         for q in range(4):
@@ -138,7 +146,7 @@ def tile_picked_actorder_lin_silu_perm_l_kernel(tc, x, w_words, w_scales, b, off
             for g in order:
                 nc.tensor.matmul_mx(
                     out=sums[blk, m][:],
-                    lhsT=w_codes[:, g, channels].bitcast(FP8X4),
+                    lhsT=w_codes[g][:, channels].bitcast(FP8X4),
                     lhsT_scale=w_planes[:, g, channels],
                     rhs=codes[blk, g].bitcast(FP8X4),
                     rhs_scale=planes[blk, g],
@@ -184,11 +192,14 @@ def tile_picked_actorder_lin_silu_perm_l_kernel(tc, x, w_words, w_scales, b, off
         turn(3, (2,), "t1")
         quantise(2, (2,))
         quantise(2, (0, 1))
-        for m in range(2):
-            finish(0, m, nc.sync)
         for g in every:
             group(3, (g,))
-            empty("scalar", 3, (g,), (g,))
+        empty("scalar", 3, (0,), (0,))
+        for m in range(2):
+            finish(0, m, nc.sync)
+        empty("vector", 3, (1,), (1,))
+        empty("scalar", 3, (2,), (2,))
+        for g in every:
             quantise(3, (g,))
         for m in range(2):
             multiply(2, m, (2, 0, 1), f"s{m}")

@@ -27,20 +27,20 @@ BLOCKS = T // P
 SHARES = [
     [("vector", 0, 0, 512), ("scalar", 1, 0, 512), ("vector", 2, 0, 256), ("scalar", 2, 256, 512)],
     [("vector", 0, 0, 512), ("scalar", 2, 0, 512), ("vector", 1, 0, 512)],
-    [("vector", 0, 0, 512), ("scalar", 2, 0, 512), ("vector", 1, 0, 384), ("scalar", 1, 384, 512)],
+    [("vector", 1, 0, 384), ("scalar", 2, 0, 512), ("vector", 0, 0, 512), ("scalar", 1, 384, 512)],
     [("scalar", 0, 0, 512), ("vector", 1, 0, 320), ("scalar", 1, 320, 512), ("vector", 2, 0, 256), ("scalar", 2, 256, 512)],
 ]
 SHARED_AT = {
     "staged0": 0,
     "grouped00": 0,
-    "landed0": 3072,
-    "grouped10": 3072,
-    "landed1": 8192 - 64,
-    "grouped20": 8192 - 2048,
-    "grouped22": 8192,
-    "picked30": 9216,
-    "result00": 9216,
-    "result10": 9216 + 512,
+    "picked20": 3072,
+    "landed0": 4096 - 64,
+    "grouped10": 4096,
+    "grouped20": 7168,
+    "landed1": 9216 - 64,
+    "grouped22": 9216,
+    "picked30": 10240,
+    "result00": 10240,
 }
 
 
@@ -81,9 +81,9 @@ def tile_picked_actorder_lin_silu_perm_l_kernel(tc, x, w_words, w_scales, b, off
                 w_scales[:, 4 * q : 4 * q + 4, :].rearrange("a q n -> q a n").bitcast(I32),
             )
         words_of_w = w_words.rearrange("a p n r -> p a (n r)").bitcast(I32)
-        nc.sync.dma_start(w_early[:].bitcast(I32), words_of_w[:, 0:LAST, :])
         load_rows(2)
         nc.sync.dma_start(landed[0][:, 0:1], b[0:P, :])
+        nc.sync.dma_start(w_early[:].bitcast(I32), words_of_w[:, 0:LAST, :])
         nc.sync.dma_start(w_late[:].bitcast(I32), words_of_w[:, LAST, :])
         load_rows(3)
         nc.sync.dma_start(landed[1][:, 0:1], b[P:N, :])
@@ -98,7 +98,7 @@ def tile_picked_actorder_lin_silu_perm_l_kernel(tc, x, w_words, w_scales, b, off
         nc.vector.memset(zero[:], 0.0)
         nc.scalar.activation(unread[:], zero[:], SILU)
 
-        picked, banks, grouped, codes, planes, sums = {}, {}, {}, {}, {}, {}
+        picked, banks, grouped, codes, planes, sums, totals = {}, {}, {}, {}, {}, {}, {}
 
         def gather(blk):
             for g in range(PASSES):
@@ -113,7 +113,7 @@ def tile_picked_actorder_lin_silu_perm_l_kernel(tc, x, w_words, w_scales, b, off
         def turn(blk, passes, tag):
             bank = psum.tile([P, HALF * len(passes)], F32, name=f"bank{blk}{passes[0]}", tag=tag)
             banks[blk, passes] = bank
-            for i, g in enumerate(passes):
+            for i, g in sorted(enumerate(passes), reverse=(blk == 2)):
                 words = picked[blk, g][:].bitcast(F32)
                 for u in range(2):
                     at = HALF * i + P * u
@@ -140,12 +140,11 @@ def tile_picked_actorder_lin_silu_perm_l_kernel(tc, x, w_words, w_scales, b, off
                 codes[blk, g] = made[:, P * i : P * (i + 1)]
                 planes[blk, g] = scales[:, P * i : P * (i + 1)]
 
-        def multiply(blk, m, order, tag):
-            sums[blk, m] = psum.tile([P, P], F32, name=f"sum{blk}{m}", tag=tag)
+        def multiply(blk, m, order):
             channels = slice(P * m, P * (m + 1))
             for g in order:
                 nc.tensor.matmul_mx(
-                    out=sums[blk, m][:],
+                    out=sums[blk, m],
                     lhsT=w_codes[g][:, channels].bitcast(FP8X4),
                     lhsT_scale=w_planes[:, g, channels],
                     rhs=codes[blk, g].bitcast(FP8X4),
@@ -154,10 +153,15 @@ def tile_picked_actorder_lin_silu_perm_l_kernel(tc, x, w_words, w_scales, b, off
                     stop=(g == order[-1]),
                 )
 
-        def finish(blk, m, queue):
-            result = sbuf(f"result{blk}{m}", [P, P], F32)
-            nc.scalar.activation(result[:], sums[blk, m][:], SILU, bias=bias[m][:])
-            queue.dma_start(out[P * m : P * (m + 1), P * blk : P * (blk + 1)], result[:])
+        def open_sums(first, blocks, m, tag):
+            totals[first, m] = psum.tile([P, P * blocks], F32, name=f"sum{first}{m}", tag=tag)
+            for e in range(blocks):
+                sums[first + e, m] = totals[first, m][:, P * e : P * (e + 1)]
+
+        def finish(first, blocks, m, queue):
+            result = sbuf(f"result{first}{m}", [P, P * blocks], F32)
+            nc.scalar.activation(result[:], totals[first, m][:], SILU, bias=bias[m][:])
+            queue.dma_start(out[P * m : P * (m + 1), P * first : P * (first + blocks)], result[:])
 
         every = (0, 1, 2)
 
@@ -175,13 +179,14 @@ def tile_picked_actorder_lin_silu_perm_l_kernel(tc, x, w_words, w_scales, b, off
         turn(1, (0, 1), "t2")
         empty_both(0)
         for m in range(2):
-            multiply(0, m, every, f"s{m}")
+            open_sums(0, 2, m, f"s{m}")
+            multiply(0, m, every)
         gather(2)
         turn(2, (2,), "t1")
         turn(2, (0, 1), "t0")
         empty_both(1)
         for m in range(2):
-            multiply(1, m, every, f"s{2 + m}")
+            multiply(1, m, every)
         gather(3)
         turn(3, (0,), "t2")
         turn(3, (1,), "t3")
@@ -195,18 +200,18 @@ def tile_picked_actorder_lin_silu_perm_l_kernel(tc, x, w_words, w_scales, b, off
         for g in every:
             group(3, (g,))
         empty("scalar", 3, (0,), (0,))
-        for m in range(2):
-            finish(0, m, nc.sync)
+        finish(0, 2, 0, nc.sync)
         empty("vector", 3, (1,), (1,))
         empty("scalar", 3, (2,), (2,))
+        finish(0, 2, 1, nc.sync)
         for g in every:
             quantise(3, (g,))
         for m in range(2):
-            multiply(2, m, (2, 0, 1), f"s{m}")
+            open_sums(2, 1, m, f"s{2 + m}")
+            multiply(2, m, (2, 0, 1))
         for m in range(2):
-            finish(1, m, nc.sync)
-        for m in range(2):
-            multiply(3, m, every, ["t0", "t2"][m])
+            open_sums(3, 1, m, ["t0", "t2"][m])
+            multiply(3, m, every)
         for blk in (2, 3):
             for m in range(2):
-                finish(blk, m, nc.scalar if (blk, m) == (3, 1) else nc.sync)
+                finish(blk, 1, m, nc.scalar if (blk, m) == (3, 1) else nc.sync)

from contextlib import ExitStack

import concourse.mybir as mybir
from concourse.masks import make_identity

K, T, N = 1536, 512, 256
FLOPS = 2 * K * T * N

F32 = mybir.dt.float32
BF16 = mybir.dt.bfloat16
U32 = mybir.dt.uint32
I32 = mybir.dt.int32
U16 = mybir.dt.uint16
U8 = mybir.dt.uint8
FP8X4 = mybir.dt.float8_e4m3fn_x4
SILU = mybir.ActivationFunctionType.Silu
COPY = mybir.ActivationFunctionType.Copy

P = 128
PACK = 4
K_PASS = P * PACK
PASSES = K // K_PASS
LAST = PASSES - 1
HALF = 2 * P
COLUMN = 16
BLOCKS = T // P
SHARES = [
    [("vector", 0, 0, 512), ("scalar", 1, 0, 512), ("vector", 2, 0, 256), ("scalar", 2, 256, 512)],
    [("vector", 0, 0, 512), ("scalar", 2, 0, 512), ("vector", 1, 0, 512)],
    [("vector", 1, 0, 384), ("scalar", 2, 0, 512), ("vector", 0, 0, 512), ("scalar", 1, 384, 512)],
    [("scalar", 0, 0, 512), ("vector", 1, 0, 320), ("scalar", 1, 320, 512), ("vector", 2, 0, 256), ("scalar", 2, 256, 512)],
]
SHARED_AT = {
    "staged0": 0,
    "grouped00": 0,
    "picked20": 3072,
    "landed0": 4096 - 64,
    "grouped10": 4096,
    "grouped20": 7168,
    "landed1": 9216 - 64,
    "grouped22": 9216,
    "picked30": 10240,
    "result00": 10240,
}


def tile_picked_actorder_lin_silu_perm_l_kernel(tc, x, w_words, w_scales, b, offs, out):
    nc = tc.nc
    with ExitStack() as ctx:
        keep = ctx.enter_context(tc.tile_pool(name="keep", bufs=1))
        psum = ctx.enter_context(tc.psum_pool(name="psum", bufs=1))
        shared = ctx.enter_context(tc.tile_pool(name="shared", bufs=1))

        def sbuf(name, shape, dtype):
            if name in SHARED_AT:
                return shared.tile(shape, dtype, name=name, align_bytes=64, offset=SHARED_AT[name])
            return keep.tile(shape, dtype, name=name, align_bytes=64)

        offsets = keep.tile([P, K // COLUMN], U16, name="offsets")
        ident = keep.tile([P, P], F32, name="ident")
        w_early = sbuf("w_early", [P, LAST, N], U32)
        w_late = sbuf("w_late", [P, N], U32)
        w_codes = [w_early[:, 0, :], w_early[:, 1, :], w_late[:]]
        w_planes = sbuf("w_planes", [P, PASSES, N], U8)
        staged = [sbuf(f"staged{q}", [P, PASSES, N], U8) for q in range(4)]
        bias = [sbuf(f"bias{m}", [P, 1], F32) for m in range(2)]
        landed = [sbuf(f"landed{m}", [P, 32], F32) for m in range(2)]
        zero = keep.tile([P, 1], F32, name="zero")
        unread = keep.tile([P, 1], F32, name="unread")
        rows = [sbuf(f"rows{blk}", [P, K], F32) for blk in range(BLOCKS)]

        def load_rows(blk):
            nc.sync.dma_start(rows[blk][:], x[P * blk : P * (blk + 1), :])

        load_rows(0)
        nc.sync.dma_start(offsets[:], offs)
        load_rows(1)
        for q in range(4):
            nc.sync.dma_start(
                staged[q][32 * q : 32 * q + 4, :, :].bitcast(I32),
                w_scales[:, 4 * q : 4 * q + 4, :].rearrange("a q n -> q a n").bitcast(I32),
            )
        words_of_w = w_words.rearrange("a p n r -> p a (n r)").bitcast(I32)
        load_rows(2)
        nc.sync.dma_start(landed[0][:, 0:1], b[0:P, :])
        nc.sync.dma_start(w_early[:].bitcast(I32), words_of_w[:, 0:LAST, :])
        nc.sync.dma_start(w_late[:].bitcast(I32), words_of_w[:, LAST, :])
        load_rows(3)
        nc.sync.dma_start(landed[1][:, 0:1], b[P:N, :])
        make_identity(nc, ident[:])
        nc.gpsimd.memset(w_planes[:].bitcast(U32), 0)
        for q in range(4):
            live = slice(32 * q, 32 * q + 4)
            nc.gpsimd.tensor_copy(w_planes[live, :, :].bitcast(I32), staged[q][live, :, :].bitcast(I32))
        for m in range(2):
            nc.gpsimd.tensor_copy(bias[m][:], landed[m][:, 0:1])

        nc.vector.memset(zero[:], 0.0)
        nc.scalar.activation(unread[:], zero[:], SILU)

        picked, banks, grouped, codes, planes, sums, totals = {}, {}, {}, {}, {}, {}, {}

        def gather(blk):
            for g in range(PASSES):
                picked[blk, g] = sbuf(f"picked{blk}{g}", [P, K_PASS], BF16)
            for engine, g, lo, hi in SHARES[blk]:
                window = rows[blk][:].indirect(offsets[:, (K_PASS * g + lo) // COLUMN : (K_PASS * g + hi) // COLUMN])
                if engine == "vector":
                    nc.vector.tensor_copy(picked[blk, g][:, lo:hi], window)
                else:
                    nc.scalar.activation(picked[blk, g][:, lo:hi], window, COPY)

        def turn(blk, passes, tag):
            bank = psum.tile([P, HALF * len(passes)], F32, name=f"bank{blk}{passes[0]}", tag=tag)
            banks[blk, passes] = bank
            for i, g in sorted(enumerate(passes), reverse=(blk == 2)):
                words = picked[blk, g][:].bitcast(F32)
                for u in range(2):
                    at = HALF * i + P * u
                    nc.tensor.transpose(bank[:, at : at + P], words[:, u:HALF:2], ident[:])

        def group(blk, passes):
            grouped[blk, passes] = sbuf(f"grouped{blk}{passes[0]}", [P, K_PASS * len(passes)], BF16)

        def empty(engine, blk, passes, into):
            first = into.index(passes[0])
            dst = grouped[blk, into][:, K_PASS * first : K_PASS * (first + len(passes))]
            dst = dst.bitcast(F32).rearrange("p (g q u) -> p g q u", g=len(passes), u=2)
            src = banks[blk, passes][:].rearrange("p (g u q) -> p g q u", g=len(passes), u=2)
            if engine == "vector":
                nc.vector.tensor_copy(dst, src)
            else:
                nc.scalar.copy(dst, src)

        def quantise(blk, passes):
            made = sbuf(f"codes{blk}{passes[0]}", [P, P * len(passes)], U32)
            scales = sbuf(f"planes{blk}{passes[0]}", [P, P * len(passes)], U8)
            nc.vector.quantize_mx(out=made[:].bitcast(FP8X4), scales=scales[:], in_=grouped[blk, passes][:])
            for i, g in enumerate(passes):
                codes[blk, g] = made[:, P * i : P * (i + 1)]
                planes[blk, g] = scales[:, P * i : P * (i + 1)]

        def multiply(blk, m, order):
            channels = slice(P * m, P * (m + 1))
            for g in order:
                nc.tensor.matmul_mx(
                    out=sums[blk, m],
                    lhsT=w_codes[g][:, channels].bitcast(FP8X4),
                    lhsT_scale=w_planes[:, g, channels],
                    rhs=codes[blk, g].bitcast(FP8X4),
                    rhs_scale=planes[blk, g],
                    start=(g == order[0]),
                    stop=(g == order[-1]),
                )

        def open_sums(first, blocks, m, tag):
            totals[first, m] = psum.tile([P, P * blocks], F32, name=f"sum{first}{m}", tag=tag)
            for e in range(blocks):
                sums[first + e, m] = totals[first, m][:, P * e : P * (e + 1)]

        def finish(first, blocks, m, queue):
            result = sbuf(f"result{first}{m}", [P, P * blocks], F32)
            nc.scalar.activation(result[:], totals[first, m][:], SILU, bias=bias[m][:])
            queue.dma_start(out[P * m : P * (m + 1), P * first : P * (first + blocks)], result[:])

        every = (0, 1, 2)

        def empty_both(blk):
            group(blk, every)
            empty("scalar", blk, (0, 1), every)
            empty("scalar", blk, (2,), every)
            quantise(blk, every)

        gather(0)
        turn(0, (0, 1), "t0")
        turn(0, (2,), "t1")
        gather(1)
        turn(1, (2,), "t3")
        turn(1, (0, 1), "t2")
        empty_both(0)
        for m in range(2):
            open_sums(0, 2, m, f"s{m}")
            multiply(0, m, every)
        gather(2)
        turn(2, (2,), "t1")
        turn(2, (0, 1), "t0")
        empty_both(1)
        for m in range(2):
            multiply(1, m, every)
        gather(3)
        turn(3, (0,), "t2")
        turn(3, (1,), "t3")
        group(2, (2,))
        empty("scalar", 2, (2,), (2,))
        group(2, (0, 1))
        empty("vector", 2, (0, 1), (0, 1))
        turn(3, (2,), "t1")
        quantise(2, (2,))
        quantise(2, (0, 1))
        for g in every:
            group(3, (g,))
        empty("scalar", 3, (0,), (0,))
        finish(0, 2, 0, nc.sync)
        empty("vector", 3, (1,), (1,))
        empty("scalar", 3, (2,), (2,))
        finish(0, 2, 1, nc.sync)
        for g in every:
            quantise(3, (g,))
        for m in range(2):
            open_sums(2, 1, m, f"s{2 + m}")
            multiply(2, m, (2, 0, 1))
        for m in range(2):
            open_sums(3, 1, m, ["t0", "t2"][m])
            multiply(3, m, every)
        for blk in (2, 3):
            for m in range(2):
                finish(blk, 1, m, nc.scalar if (blk, m) == (3, 1) else nc.sync)
